import numpy as np
import ml_dtypes


def mxq(x, axis, fmt="e4m3"):
    dtype, down = {"e4m3": (ml_dtypes.float8_e4m3fn, 7), "e5m2": (ml_dtypes.float8_e5m2, 14)}[fmt]
    v = np.moveaxis(np.asarray(x, np.float32).astype(ml_dtypes.bfloat16).astype(np.float64), axis, -1)
    blocks = v.reshape(v.shape[:-1] + (-1, 32))
    amax = np.abs(blocks).max(-1, keepdims=True)
    byte = np.maximum(np.where(amax > 0, np.frexp(amax)[1] - 1 + 127, 0) - down, 1)
    scale = np.exp2(byte - 127.0)
    codes = (blocks / scale).astype(np.float32).astype(dtype).astype(np.float64)
    return np.moveaxis((codes * scale).reshape(v.shape), -1, axis)


WIDE = False


def mx_kscale(k):
    if not WIDE:
        return np.ones(k)
    levels = np.array([10, -10, 5, -5, 0])
    if k % 512:
        return np.exp2(np.random.permutation(np.resize(levels, k // 32))).repeat(32)
    a = np.empty((k // 512, 16))
    for p in range(k // 512):
        a[p, :8] = np.random.permutation(np.resize(levels, 8))
        for g in range(8):
            far = levels[np.abs(levels - a[p, g]) >= 10]
            a[p, g + 8] = far[np.random.randint(len(far))]
    return np.exp2(a.ravel()).repeat(32)


BF16 = ml_dtypes.bfloat16


def bf(x):
    return np.asarray(x, np.float32).astype(BF16)


def f64(x):
    return np.asarray(x).astype(np.float64)


E2M1 = np.array([0.0, 0.5, 1.0, 1.5, 2.0, 3.0, 4.0, 6.0, -0.0, -0.5, -1.0, -1.5, -2.0, -3.0, -4.0, -6.0])


def pack_weight(w, fmt):
    k, n = w.shape
    w = f64(bf(w)).reshape(k // 32, 32, n)
    amax = np.abs(w).max(1)
    if fmt == "e4m3":
        byte = np.frexp(amax)[1] - 1 + 127 - 7
    else:
        mant, ex = np.frexp(amax / 6.0)
        byte = np.where(mant > 0.5, ex, ex - 1) + 127
    byte = np.clip(np.where(amax > 0, byte, 1), 1, 254)
    scaled = (w * np.exp2(127.0 - byte)[:, None, :]).reshape(k, n).astype(np.float32)
    by_word = np.ascontiguousarray(scaled.reshape(k // 512, 128, 4, n).transpose(0, 1, 3, 2))
    if fmt == "e4m3":
        words = by_word.astype(ml_dtypes.float8_e4m3fn).view(np.uint8)
    else:
        c = by_word.astype(ml_dtypes.float4_e2m1fn).view(np.uint8) & 0xF
        words = c[..., 0::2] | (c[..., 1::2] << 4)
    return np.ascontiguousarray(words), np.ascontiguousarray(byte.astype(np.uint8).reshape(k // 512, 16, n))


def unpack_weight(words, scales, fmt):
    g, p, n, _ = words.shape
    if fmt == "e4m3":
        vals = np.ascontiguousarray(words).view(ml_dtypes.float8_e4m3fn).astype(np.float64)
    else:
        nib = np.empty((g, p, n, 4), np.uint8)
        nib[..., 0::2] = words & 0xF
        nib[..., 1::2] = words >> 4
        vals = E2M1[nib]
    vals = vals * np.repeat(np.exp2(scales.astype(np.float64) - 127.0), 8, axis=1)[..., None]
    return vals.transpose(0, 1, 3, 2).reshape(g * 512, n)
def pack4(w):
    words, scales = pack_weight(w, "e2m1")
    return words.reshape(words.shape[0], 128, -1), scales


def unpack4(words, scales):
    return unpack_weight(words.reshape(words.shape[0], 128, -1, 2), scales, "e2m1")


I, J, C, K, R = 1024, 1024, 2, 1024, 512


def setup_inputs():
    s = mx_kscale(K)
    t = mx_kscale(C * J)
    u = mx_kscale(I)
    left = np.random.standard_normal((I, K)) * s * u[:, None]
    right = np.random.standard_normal((C * J, K)) / np.sqrt(K) / s * t[:, None]
    prior = 0.5 * np.random.standard_normal((I, C * J)) * u[:, None] * t
    near = np.random.uniform(0.2, 1.8, (I, J))
    v = np.random.standard_normal((C * J, R)) / np.sqrt(C * J) / t[:, None]
    y = np.random.standard_normal((I, R)) / np.sqrt(I) / u[:, None]
    v_words, v_scales = pack4(v)
    return {"left": bf(left), "right": bf(right), "prior": bf(prior), "near": bf(near),
            "v_words": v_words, "v_scales": v_scales, "y": bf(y)}


def reference(left, right, prior, near, v_words, v_scales, y):
    z = mxq(f64(left), 1, "e4m3") @ mxq(f64(right), 1, "e4m3").T
    z = np.maximum(z + f64(prior), 0.0)
    z = (z.reshape(I, C, J) * f64(near)[:, None, :]).reshape(I, C * J)
    to_ligand = mxq(z, 1, "e4m3") @ unpack4(v_words, v_scales)
    to_receptor = mxq(z, 0, "e4m3").T @ mxq(f64(y), 0, "e4m3")
    return to_ligand, to_receptor

@@ -1,0 +1,521 @@
+from contextlib import ExitStack
+
+import concourse.mybir as mybir
+from concourse.masks import make_identity
+
+F32 = mybir.dt.float32
+BF16 = mybir.dt.bfloat16
+I32 = mybir.dt.int32
+U32 = mybir.dt.uint32
+U8 = mybir.dt.uint8
+FP8X4 = mybir.dt.float8_e4m3fn_x4
+FP4X4 = mybir.dt.float4_e2m1fn_x4
+ALU = mybir.AluOpType
+
+I, J, C, K, R = 1024, 1024, 2, 1024, 512
+M = C * J
+P = 128
+PACK = 4
+SPAN = P * PACK
+K_PASSES = K // SPAN
+LIG = I // SPAN
+REC = M // SPAN
+FLOPS = 2 * I * M * K + 2 * I * M * R + 2 * M * I * R
+
+ZI_BUFS, ZM_BUFS = 5, 6
+
+
+def tile_pair_tensor_messages_s8_kernel(tc, left, right, prior, near, v_words, v_scales, y, out_0, out_1):
+    nc = tc.nc
+    with ExitStack() as ctx:
+        keep = ctx.enter_context(tc.tile_pool(name="keep", bufs=1))
+        ring = ctx.enter_context(tc.tile_pool(name="ring", bufs=2))
+        psum = ctx.enter_context(tc.psum_pool(name="psum", bufs=1))
+        ctx.enter_context(tc.manual_schedule())
+
+        def bank(n):
+            return psum.tile([P, SPAN], F32, name="bank%d" % n)
+
+        ident = keep.tile([P, P], F32, name="ident")
+        make_identity(nc, ident[:])
+        v_codes = keep.tile([P, REC, 2 * R], U8, name="v_codes", align_bytes=64)
+        v_plane = keep.tile([P, REC, R], U8, name="v_plane", align_bytes=64)
+        nc.vector.memset(v_plane[:].bitcast(I32), 0)
+
+        raw, staged, codes, scales, acc = {}, {}, {}, {}, {}
+        prior_sb, near_sb, y_raw, y_staged = {}, {}, {}, {}
+        summed, paired, along_i, along_m = {}, {}, {}, {}
+
+        def rows(src, n):
+            return src[n * SPAN:(n + 1) * SPAN, :].rearrange("(p t) d -> p t d", t=PACK)
+
+        def span(n, width):
+            return slice(n * width, (n + 1) * width)
+
+        def load_proj(key, lo, hi):
+            if key not in raw:
+                raw[key] = ring.tile([P, PACK, K], BF16, name="raw", bufs=4)
+            src = left if key[0] == "left" else right
+            nc.sync.dma_start(out=raw[key][:, lo:hi, :], in_=rows(src, key[1])[:, lo:hi, :])
+
+        def load_prior(b, lo=0, hi=PACK):
+            if b not in prior_sb:
+                prior_sb[b] = ring.tile([P, PACK, SPAN], BF16, name="prior_sb", bufs=4)
+            nc.sync.dma_start(out=prior_sb[b][:, lo:hi, :], in_=rows(prior, b[0])[:, lo:hi, span(b[1], SPAN)])
+
+        def load_near(b, lo=0, hi=PACK):
+            key = (b[0], b[1] % C)
+            if key not in near_sb:
+                near_sb[key] = keep.tile([P, PACK, SPAN], BF16, name="near%d%d" % key)
+            nc.sync.dma_start(out=near_sb[key][:, lo:hi, :], in_=rows(near, key[0])[:, lo:hi, span(key[1], SPAN)])
+
+        def load_y(g, lo=0, hi=PACK):
+            if g not in y_raw:
+                y_raw[g] = ring.tile([P, PACK, R], BF16, name="y_raw")
+            nc.sync.dma_start(out=y_raw[g][:, :, lo * P:hi * P], in_=rows(y, g)[:, :, lo * P:hi * P])
+
+        def load_v():
+            for r in range(PACK):
+                nc.sync.dma_start(out=v_plane[r:P:32, :, :].bitcast(I32),
+                                  in_=v_scales[:, r:16:PACK, :].rearrange("g q n -> q g n").bitcast(I32))
+            nc.sync.dma_start(out=v_codes[:].bitcast(I32), in_=v_words.rearrange("g p n -> p g n").bitcast(I32))
+
+        def quantize(key, src, cols, bufs):
+            if key not in codes:
+                width = src.shape[1] // PACK
+                codes[key] = ring.tile([P, width], U32, name=key[0] + "_codes", bufs=bufs, align_bytes=64)
+                scales[key] = ring.tile([P, width], U8, name=key[0] + "_scales", bufs=bufs, align_bytes=64)
+            nc.vector.quantize_mx(out=codes[key][:, cols].bitcast(FP8X4), scales=scales[key][:, cols],
+                                  in_=src[:, PACK * cols.start:PACK * cols.stop])
+
+        def pieces(key, quarter):
+            if key[0] == "left":
+                return [(quarter, kk) for kk in range(K_PASSES)]
+            return [(2 * (quarter // 2) + a, quarter % 2) for a in range(2)]
+
+        def place(key, quarter):
+            return quarter if key[0] == "left" else 2 * (quarter % 2) + quarter // 2
+
+        def turn_proj(key, quarter, n):
+            acc[key, quarter] = bank(n)
+            for a, (slot, kk) in enumerate(pieces(key, quarter)):
+                words = raw[key][:, slot, :].bitcast(F32)
+                for u in range(2):
+                    nc.tensor.transpose(acc[key, quarter][:, span(2 * a + u, P)],
+                                        words[:, 2 * P * kk + u:2 * P * (kk + 1):2], ident[:])
+
+        def stage_proj(key, quarter):
+            if key not in staged:
+                staged[key] = ring.tile([P, K_PASSES * SPAN * PACK], BF16, name="staged", align_bytes=64)
+            dst = staged[key][:].bitcast(F32)[:, span(place(key, quarter), SPAN)]
+            nc.scalar.copy(out=dst.rearrange("p (a r u) -> p a r u", a=2, u=2),
+                           in_=acc[key, quarter][:].rearrange("p (a u r) -> p a r u", a=2, u=2))
+
+        def quantize_proj(key, lo, hi):
+            quantize(key, staged[key], slice(2 * P * lo, 2 * P * hi), LIG if key[0] == "left" else REC)
+
+        def mx(out, a, a_cols, b, b_cols, start, stop):
+            nc.tensor.matmul_mx(out=out[:], lhsT=codes[a][:, a_cols].bitcast(FP8X4), lhsT_scale=scales[a][:, a_cols],
+                                rhs=codes[b][:, b_cols].bitcast(FP8X4), rhs_scale=scales[b][:, b_cols],
+                                start=start, stop=stop)
+
+        def pair_matmul(b, t, n):
+            acc[b, t] = bank(n)
+            for kk in range(K_PASSES):
+                mx(acc[b, t], ("left", b[0]), span(K_PASSES * t + kk, P), ("right", b[1]), span(kk, SPAN),
+                   kk == 0, kk == K_PASSES - 1)
+
+        def add_prior(b, t):
+            if b not in summed:
+                summed[b] = ring.tile([P, PACK, SPAN], F32, name="summed")
+            nc.vector.tensor_tensor(out=summed[b][:, t, :].rearrange("p (s q) -> p s q", s=PACK),
+                                    in0=acc[b, t][:].rearrange("p (s q) -> p s q", s=PACK),
+                                    in1=prior_sb[b][:, t, :].rearrange("p (q s) -> p s q", s=PACK), op=ALU.add)
+
+        def gate(b, u, lo, hi):
+            if b not in paired:
+                paired[b] = ring.tile([P, 2, 2 * SPAN], BF16, name="paired", bufs=3)
+            for s in range(lo, hi):
+                nc.vector.scalar_tensor_tensor(
+                    out=paired[b][:, u, span(s, 2 * P)].rearrange("p (q e) -> p q e", e=2),
+                    in0=summed[b][:, span(u, 2), span(s, P)].rearrange("p e q -> p q e"), scalar=0.0,
+                    in1=near_sb[b[0], b[1] % C][:, span(u, 2), s:SPAN:PACK].rearrange("p e q -> p q e"),
+                    op0=ALU.max, op1=ALU.mult)
+
+        def turn_pair(b, u, n):
+            acc[b, "turned", u] = bank(n)
+            words = paired[b][:].bitcast(F32)
+            for s in range(PACK):
+                nc.tensor.transpose(acc[b, "turned", u][:, span(s, P)], words[:, u, span(s, P)], ident[:])
+
+        def stage_along_m(b, u):
+            if b not in along_m:
+                along_m[b] = ring.tile([P, SPAN * PACK], BF16, name="along_m", align_bytes=64)
+            nc.scalar.copy(out=along_m[b][:, span(u, 2 * SPAN)].rearrange("q (e p s) -> q e p s", e=2, s=PACK),
+                           in_=acc[b, "turned", u][:].bitcast(BF16).rearrange("q (s p e) -> q e p s", s=PACK, e=2))
+
+        def stage_along_i(b, lo, hi, copy):
+            if b not in along_i:
+                along_i[b] = ring.tile([P, SPAN * PACK], BF16, name="along_i", align_bytes=64)
+            cols = slice(lo * P, hi * P)
+            copy(out=along_i[b][:].bitcast(F32).rearrange("p (c u) -> p c u", u=2)[:, cols, :],
+                 in_=paired[b][:].bitcast(F32).rearrange("p u c -> p c u")[:, cols, :])
+
+        def quantize_along_i(b, lo, hi):
+            quantize(("zi", b), along_i[b], slice(lo * P, hi * P), ZI_BUFS)
+
+        def quantize_along_m(b, lo, hi):
+            quantize(("zm", b), along_m[b], slice(lo * P, hi * P), ZM_BUFS)
+
+        def stage_y(g, lo, hi, copy):
+            if g not in y_staged:
+                y_staged[g] = ring.tile([P, R * PACK], BF16, name="y_staged", align_bytes=64)
+            cols = slice(lo * P, hi * P)
+            copy(out=y_staged[g][:].rearrange("p (r t) -> p r t", t=PACK)[:, cols, :],
+                 in_=y_raw[g][:].rearrange("p t r -> p r t")[:, cols, :])
+
+        def quantize_y(g, lo=0, hi=PACK):
+            quantize(("y", g), y_staged[g], slice(lo * P, hi * P), LIG)
+
+        def keep_busy(count, key, width, n):
+            idle = bank(n)
+            for repeat in range(count):
+                mx(idle[:, 0:width], key, slice(0, P), key, slice(0, width), True, True)
+
+        def ligand_passes(g, t, chunks, start, stop, own_bank=None):
+            if start:
+                acc["lig", g, t] = bank(own_bank)
+            for n in chunks:
+                key = ("zm", (g, n))
+                nc.tensor.matmul_mx(out=acc["lig", g, t][:], lhsT=codes[key][:, span(t, P)].bitcast(FP8X4),
+                                    lhsT_scale=scales[key][:, span(t, P)],
+                                    rhs=v_codes[:, n, :].bitcast(FP4X4), rhs_scale=v_plane[:, n, :],
+                                    start=start and n == chunks[0], stop=stop and n == chunks[-1])
+
+        def receptor_passes(n, s, own_bank):
+            acc["rec", n, s] = bank(own_bank)
+            for g in range(LIG):
+                mx(acc["rec", n, s], ("zi", (g, n)), span(s, P), ("y", g), slice(0, R), g == 0, g == LIG - 1)
+
+        def emit(kind, n, slot, copy):
+            res = ring.tile([P, R], F32, name="res", bufs=8)
+            copy(out=res[:], in_=acc[kind, n, slot][:])
+            nc.sync.dma_start(out=rows(out_0 if kind == "lig" else out_1, n)[:, slot, :], in_=res[:])
+
+        on_scalar, on_vector = nc.scalar.copy, nc.vector.tensor_copy
+
+        def on_gpsimd(out, in_):
+            nc.gpsimd.tensor_scalar(out=out, in0=in_, scalar1=1.0, scalar2=0.0, op0=ALU.mult, op1=ALU.add)
+
+        def stage_along_i_gpsimd(b, lo, hi):
+            if b not in along_i:
+                along_i[b] = ring.tile([P, SPAN * PACK], BF16, name="along_i", align_bytes=64)
+            cols = slice(lo * P, hi * P)
+            on_gpsimd(along_i[b][:].rearrange("p (c u e) -> p c u e", u=2, e=2)[:, cols, :, :],
+                      paired[b][:].rearrange("p u (c e) -> p c u e", e=2)[:, cols, :, :])
+
+        load_proj(("right", 0), 0, 2)
+        turn_proj(("right", 0), 0, 7)
+        stage_proj(("right", 0), 0)
+        load_proj(("right", 0), 2, 4)
+        turn_proj(("right", 0), 1, 1)
+        stage_proj(("right", 0), 1)
+        turn_proj(("right", 0), 2, 0)
+        load_proj(("left", 0), 0, 2)
+        turn_proj(("right", 0), 3, 7)
+        turn_proj(("left", 0), 0, 1)
+        stage_proj(("right", 0), 2)
+        turn_proj(("left", 0), 1, 2)
+        load_proj(("left", 0), 2, 4)
+        turn_proj(("left", 0), 2, 4)
+        quantize_proj(("right", 0), 2, 3)
+        load_y(0)
+        stage_proj(("right", 0), 3)
+        load_prior((0, 0))
+        quantize_proj(("right", 0), 3, 4)
+        load_proj(("right", 2), 0, 2)
+        quantize_proj(("right", 0), 1, 2)
+        stage_proj(("left", 0), 0)
+        quantize_proj(("right", 0), 0, 1)
+        stage_proj(("left", 0), 1)
+        quantize_proj(("left", 0), 0, 1)
+        turn_proj(("left", 0), 3, 0)
+        stage_proj(("left", 0), 2)
+        pair_matmul((0, 0), 0, 5)
+        quantize_proj(("left", 0), 2, 3)
+        stage_proj(("left", 0), 3)
+        quantize_proj(("left", 0), 1, 2)
+        stage_y(0, 0, 2, on_scalar)
+        pair_matmul((0, 0), 1, 0)
+        pair_matmul((0, 0), 2, 1)
+        quantize_proj(("left", 0), 3, 4)
+        load_near((0, 0), 0, 2)
+        pair_matmul((0, 0), 3, 4)
+        turn_proj(("right", 2), 0, 3)
+        add_prior((0, 0), 0)
+        load_proj(("right", 2), 2, 4)
+        stage_y(0, 2, 4, on_scalar)
+        add_prior((0, 0), 1)
+        load_proj(("left", 1), 0, 2)
+        add_prior((0, 0), 2)
+        turn_proj(("right", 2), 1, 2)
+        turn_proj(("right", 2), 2, 0)
+        stage_proj(("right", 2), 0)
+        turn_proj(("right", 2), 3, 1)
+        load_near((0, 0), 2, 4)
+        stage_proj(("right", 2), 1)
+        load_y(1)
+        stage_proj(("right", 2), 2)
+        gate((0, 0), 0, 0, 4)
+        add_prior((0, 0), 3)
+        quantize_y(0)
+        turn_pair((0, 0), 0, 6)
+        stage_proj(("right", 2), 3)
+        turn_proj(("left", 1), 1, 4)
+        quantize_proj(("right", 2), 0, 2)
+        stage_proj(("left", 1), 1)
+        turn_proj(("left", 1), 0, 3)
+        quantize_proj(("right", 2), 2, 4)
+        pair_matmul((0, 2), 1, 1)
+        pair_matmul((0, 2), 3, 7)
+        stage_proj(("left", 1), 0)
+        pair_matmul((0, 2), 0, 3)
+        stage_along_m((0, 0), 0)
+        load_prior((0, 2))
+        gate((0, 0), 1, 0, 4)
+        quantize_proj(("left", 1), 0, 2)
+        pair_matmul((0, 2), 2, 6)
+        load_proj(("left", 1), 2, 4)
+        turn_proj(("left", 1), 3, 0)
+        add_prior((0, 2), 1)
+        stage_along_i((0, 0), 0, 1, on_scalar)
+        load_proj(("right", 1), 0, 4)
+        add_prior((0, 2), 3)
+        stage_y(1, 2, 4, on_scalar)
+        stage_along_i_gpsimd((0, 0), 1, 4)
+        add_prior((0, 2), 0)
+        add_prior((0, 2), 2)
+        quantize_along_i((0, 0), 0, 4)
+        gate((0, 2), 1, 0, 4)
+        stage_proj(("left", 1), 3)
+        turn_proj(("left", 1), 2, 4)
+        load_near((1, 0))
+        stage_proj(("left", 1), 2)
+        turn_pair((0, 0), 1, 2)
+        pair_matmul((1, 0), 0, 5)
+        stage_along_m((0, 0), 1)
+        stage_y(1, 0, 2, on_scalar)
+        load_prior((1, 0))
+        quantize_proj(("left", 1), 2, 4)
+        turn_proj(("right", 1), 1, 6)
+        load_proj(("right", 3), 0, 4)
+        turn_proj(("right", 1), 2, 7)
+        gate((0, 2), 0, 0, 4)
+        turn_proj(("right", 1), 0, 3)
+        turn_proj(("right", 1), 3, 4)
+        stage_proj(("right", 1), 2)
+        stage_proj(("right", 1), 1)
+        pair_matmul((1, 0), 2, 2)
+        pair_matmul((1, 0), 1, 0)
+        quantize_along_m((0, 0), 0, 4)
+        add_prior((1, 0), 0)
+        add_prior((1, 0), 2)
+        stage_along_i_gpsimd((0, 2), 1, 4)
+        stage_proj(("right", 1), 0)
+        pair_matmul((1, 0), 3, 7)
+        turn_pair((0, 2), 1, 6)
+        add_prior((1, 0), 1)
+        turn_pair((0, 2), 0, 1)
+        turn_proj(("right", 3), 3, 2)
+        add_prior((1, 0), 3)
+        load_v()
+        quantize_proj(("right", 1), 0, 2)
+        stage_along_i((0, 2), 0, 1, on_scalar)
+        load_prior((0, 1))
+        stage_proj(("right", 1), 3)
+        turn_proj(("right", 3), 0, 4)
+        quantize_proj(("right", 1), 2, 4)
+        gate((1, 0), 0, 0, 4)
+        gate((1, 0), 1, 0, 4)
+        quantize_y(1)
+        turn_proj(("right", 3), 1, 3)
+        pair_matmul((0, 1), 1, 5)
+        stage_along_m((0, 2), 1)
+        stage_proj(("right", 3), 0)
+        stage_proj(("right", 3), 1)
+        pair_matmul((0, 1), 2, 0)
+        load_prior((1, 3))
+        pair_matmul((0, 1), 0, 6)
+        turn_pair((1, 0), 0, 7)
+        stage_proj(("right", 3), 3)
+        add_prior((0, 1), 0)
+        add_prior((0, 1), 1)
+        stage_along_m((0, 2), 0)
+        turn_proj(("right", 3), 2, 3)
+        stage_along_i((1, 0), 0, 1, on_scalar)
+        load_near((0, 1))
+        stage_along_i_gpsimd((1, 0), 1, 4)
+        turn_pair((1, 0), 1, 2)
+        pair_matmul((0, 1), 3, 4)
+        load_near((1, 1))
+        stage_along_m((1, 0), 0)
+        load_prior((0, 3))
+        keep_busy(3, ("right", 0), 512, 1)
+        add_prior((0, 1), 2)
+        load_prior((1, 2))
+        pair_matmul((1, 2), 2, 7)
+        add_prior((0, 1), 3)
+        stage_proj(("right", 3), 2)
+        quantize_along_i((1, 0), 0, 4)
+        gate((0, 1), 0, 0, 4)
+        load_prior((1, 1))
+        gate((0, 1), 1, 0, 4)
+        quantize_proj(("right", 3), 0, 2)
+        pair_matmul((1, 2), 3, 6)
+        stage_along_m((1, 0), 1)
+        quantize_proj(("right", 3), 2, 4)
+        receptor_passes(0, 0, 5)
+        emit("rec", 0, 0, on_scalar)
+        receptor_passes(0, 2, 3)
+        receptor_passes(0, 3, 0)
+        quantize_along_i((0, 2), 0, 4)
+        quantize_along_m((0, 2), 0, 4)
+        turn_pair((0, 1), 0, 1)
+        emit("rec", 0, 2, on_scalar)
+        turn_pair((0, 1), 1, 2)
+        emit("rec", 0, 3, on_scalar)
+        receptor_passes(0, 1, 4)
+        pair_matmul((0, 3), 3, 3)
+        add_prior((0, 3), 3)
+        pair_matmul((0, 3), 0, 0)
+        pair_matmul((0, 3), 1, 5)
+        add_prior((0, 3), 0)
+        emit("rec", 0, 1, on_scalar)
+        pair_matmul((0, 3), 2, 4)
+        pair_matmul((1, 1), 3, 3)
+        stage_along_i_gpsimd((0, 1), 1, 4)
+        add_prior((0, 3), 1)
+        pair_matmul((1, 2), 1, 0)
+        stage_along_i((0, 1), 0, 1, on_scalar)
+        add_prior((1, 2), 2)
+        stage_along_m((0, 1), 1)
+        pair_matmul((1, 2), 0, 2)
+        gate((0, 3), 0, 0, 4)
+        add_prior((0, 3), 2)
+        quantize_along_m((1, 0), 0, 4)
+        turn_pair((0, 3), 0, 7)
+        stage_along_m((0, 1), 0)
+        gate((0, 3), 1, 0, 4)
+        stage_along_m((0, 3), 0)
+        pair_matmul((1, 1), 2, 1)
+        quantize_along_m((0, 1), 0, 4)
+        pair_matmul((1, 3), 1, 5)
+        stage_along_i((0, 3), 0, 1, on_scalar)
+        turn_pair((0, 3), 1, 4)
+        stage_along_m((0, 3), 1)
+        add_prior((1, 1), 2)
+        stage_along_i_gpsimd((0, 3), 1, 4)
+        add_prior((1, 2), 0)
+        ligand_passes(0, 1, [0, 2, 1], True, False, 7)
+        pair_matmul((1, 1), 0, 1)
+        add_prior((1, 2), 1)
+        add_prior((1, 2), 3)
+        ligand_passes(0, 2, [0, 2, 1], True, False, 4)
+        quantize_along_m((0, 3), 0, 4)
+        ligand_passes(0, 0, [0, 2, 1], True, False, 2)
+        gate((1, 2), 0, 0, 4)
+        quantize_along_i((0, 1), 0, 4)
+        ligand_passes(0, 0, [3], False, True)
+        emit("lig", 0, 0, on_scalar)
+        ligand_passes(0, 2, [3], False, True)
+        emit("lig", 0, 2, on_scalar)
+        ligand_passes(0, 1, [3], False, True)
+        ligand_passes(0, 3, [0, 2, 1, 3], True, True, 6)
+        emit("lig", 0, 1, on_scalar)
+        emit("lig", 0, 3, on_scalar)
+        pair_matmul((1, 1), 1, 2)
+        gate((1, 2), 1, 0, 4)
+        add_prior((1, 1), 0)
+        stage_along_i_gpsimd((1, 2), 1, 4)
+        turn_pair((1, 2), 0, 4)
+        add_prior((1, 1), 3)
+        add_prior((1, 3), 1)
+        turn_pair((1, 2), 1, 6)
+        pair_matmul((1, 3), 2, 0)
+        pair_matmul((1, 3), 0, 1)
+        stage_along_i((1, 2), 0, 1, on_scalar)
+        stage_along_m((1, 2), 1)
+        add_prior((1, 1), 1)
+        pair_matmul((1, 3), 3, 3)
+        gate((1, 1), 1, 2, 4)
+        quantize_along_i((1, 2), 0, 4)
+        receptor_passes(2, 0, 7)
+        gate((1, 1), 1, 0, 2)
+        receptor_passes(2, 3, 5)
+        stage_along_m((1, 2), 0)
+        emit("rec", 2, 0, on_scalar)
+        receptor_passes(2, 2, 6)
+        gate((1, 1), 0, 0, 4)
+        emit("rec", 2, 3, on_scalar)
+        receptor_passes(2, 1, 7)
+        quantize_along_i((0, 3), 0, 4)
+        emit("rec", 2, 2, on_scalar)
+        add_prior((1, 3), 0)
+        emit("rec", 2, 1, on_scalar)
+        quantize_along_m((1, 2), 0, 4)
+        add_prior((1, 3), 3)
+        add_prior((1, 3), 2)
+        stage_along_i((1, 1), 0, 2, on_scalar)
+        stage_along_i((1, 1), 2, 4, on_scalar)
+        turn_pair((1, 1), 0, 5)
+        turn_pair((1, 1), 1, 2)
+        quantize_along_i((1, 1), 0, 4)
+        gate((1, 3), 1, 0, 2)
+        ligand_passes(1, 0, [0, 2], True, False, 6)
+        stage_along_m((1, 1), 1)
+        gate((1, 3), 0, 0, 2)
+        ligand_passes(1, 1, [0, 2], True, False, 7)
+        ligand_passes(1, 3, [0, 2], True, False, 1)
+        receptor_passes(1, 3, 4)
+        stage_along_m((1, 1), 0)
+        emit("rec", 1, 3, on_vector)
+        stage_along_i((1, 3), 0, 2, on_scalar)
+        gate((1, 3), 1, 2, 4)
+        receptor_passes(1, 0, 3)
+        receptor_passes(1, 2, 0)
+        emit("rec", 1, 0, on_scalar)
+        gate((1, 3), 0, 2, 4)
+        receptor_passes(1, 1, 5)
+        turn_pair((1, 3), 1, 2)
+        quantize_along_i((1, 3), 0, 2)
+        turn_pair((1, 3), 0, 4)
+        emit("rec", 1, 1, on_scalar)
+        emit("rec", 1, 2, on_scalar)
+        stage_along_m((1, 3), 0)
+        stage_along_i((1, 3), 2, 4, on_vector)
+        receptor_passes(3, 1, 3)
+        quantize_along_m((1, 1), 0, 4)
+        receptor_passes(3, 0, 5)
+        ligand_passes(1, 2, [0, 2], True, False, 0)
+        emit("rec", 3, 1, on_vector)
+        quantize_along_i((1, 3), 2, 4)
+        receptor_passes(3, 2, 3)
+        ligand_passes(1, 1, [1], False, False)
+        emit("rec", 3, 0, on_scalar)
+        stage_along_m((1, 3), 1)
+        quantize_along_m((1, 3), 0, 2)
+        ligand_passes(1, 1, [3], False, True)
+        receptor_passes(3, 3, 5)
+        emit("rec", 3, 2, on_vector)
+        emit("lig", 1, 1, on_vector)
+        quantize_along_m((1, 3), 2, 4)
+        ligand_passes(1, 0, [1], False, False)
+        ligand_passes(1, 0, [3], False, True)
+        emit("rec", 3, 3, on_scalar)
+        ligand_passes(1, 2, [1], False, False)
+        emit("lig", 1, 0, on_vector)
+        ligand_passes(1, 2, [3], False, True)
+        emit("lig", 1, 2, on_vector)
+        ligand_passes(1, 3, [1], False, False)
+        ligand_passes(1, 3, [3], False, True)
+        emit("lig", 1, 3, on_scalar)

@@ -126,10 +126,23 @@ def tile_pair_tensor_messages_s8_kernel(tc, left, right, prior, near, v_words, v
                    kk == 0, kk == K_PASSES - 1)
 
         def add_prior(b, t):
-            if b not in summed:
-                summed[b] = ring.tile([P, PACK, SPAN], F32, name="summed")
-            nc.vector.tensor_tensor(out=summed[b][:, t, :].rearrange("p (s q) -> p s q", s=PACK),
+            if (b, t // 2) not in summed:
+                summed[b, t // 2] = ring.tile([P, 2, SPAN], F32, name="summed%d" % (t // 2), bufs=2 - t // 2)
+            nc.vector.tensor_tensor(out=summed[b, t // 2][:, t % 2, :].rearrange("p (s q) -> p s q", s=PACK),
                                     in0=acc[b, t][:].rearrange("p (s q) -> p s q", s=PACK),
+                                    in1=prior_sb[b][:, t, :].rearrange("p (q s) -> p s q", s=PACK), op=ALU.add)
+
+        spilled = {}
+
+        def spill(b, t):
+            spilled[b] = ring.tile([P, SPAN], F32, name="spilled")
+            nc.scalar.copy(out=spilled[b][:], in_=acc[b, t][:])
+
+        def add_prior_gpsimd(b, t):
+            if (b, t // 2) not in summed:
+                summed[b, t // 2] = ring.tile([P, 2, SPAN], F32, name="summed%d" % (t // 2), bufs=2 - t // 2)
+            nc.gpsimd.tensor_tensor(out=summed[b, t // 2][:, t % 2, :].rearrange("p (s q) -> p s q", s=PACK),
+                                    in0=spilled[b][:].rearrange("p (s q) -> p s q", s=PACK),
                                     in1=prior_sb[b][:, t, :].rearrange("p (q s) -> p s q", s=PACK), op=ALU.add)
 
         def gate(b, u, lo, hi):
@@ -138,7 +151,7 @@ def tile_pair_tensor_messages_s8_kernel(tc, left, right, prior, near, v_words, v
             for s in range(lo, hi):
                 nc.vector.scalar_tensor_tensor(
                     out=paired[b][:, u, span(s, 2 * P)].rearrange("p (q e) -> p q e", e=2),
-                    in0=summed[b][:, span(u, 2), span(s, P)].rearrange("p e q -> p q e"), scalar=0.0,
+                    in0=summed[b, u][:, :, span(s, P)].rearrange("p e q -> p q e"), scalar=0.0,
                     in1=near_sb[b[0], b[1] % C][:, span(u, 2), s:SPAN:PACK].rearrange("p e q -> p q e"),
                     op0=ALU.max, op1=ALU.mult)
 
@@ -157,7 +170,7 @@ def tile_pair_tensor_messages_s8_kernel(tc, left, right, prior, near, v_words, v
         def stage_along_i(b, lo, hi, copy):
             if b not in along_i:
                 along_i[b] = ring.tile([P, SPAN * PACK], BF16, name="along_i", align_bytes=64)
-            cols = slice(lo * P, hi * P)
+            cols = slice(int(lo * P), int(hi * P))
             copy(out=along_i[b][:].bitcast(F32).rearrange("p (c u) -> p c u", u=2)[:, cols, :],
                  in_=paired[b][:].bitcast(F32).rearrange("p u c -> p c u")[:, cols, :])
 
@@ -210,311 +223,308 @@ def tile_pair_tensor_messages_s8_kernel(tc, left, right, prior, near, v_words, v
         def stage_along_i_gpsimd(b, lo, hi):
             if b not in along_i:
                 along_i[b] = ring.tile([P, SPAN * PACK], BF16, name="along_i", align_bytes=64)
-            cols = slice(lo * P, hi * P)
+            cols = slice(int(lo * P), int(hi * P))
             on_gpsimd(along_i[b][:].rearrange("p (c u e) -> p c u e", u=2, e=2)[:, cols, :, :],
                       paired[b][:].rearrange("p u (c e) -> p c u e", e=2)[:, cols, :, :])
 
         load_proj(("right", 0), 0, 2)
-        turn_proj(("right", 0), 0, 7)
-        stage_proj(("right", 0), 0)
         load_proj(("right", 0), 2, 4)
-        turn_proj(("right", 0), 1, 1)
-        stage_proj(("right", 0), 1)
-        turn_proj(("right", 0), 2, 0)
+        turn_proj(("right", 0), 0, 0)
         load_proj(("left", 0), 0, 2)
-        turn_proj(("right", 0), 3, 7)
-        turn_proj(("left", 0), 0, 1)
-        stage_proj(("right", 0), 2)
-        turn_proj(("left", 0), 1, 2)
         load_proj(("left", 0), 2, 4)
-        turn_proj(("left", 0), 2, 4)
-        quantize_proj(("right", 0), 2, 3)
+        stage_proj(("right", 0), 0)
+        turn_proj(("right", 0), 1, 7)
+        stage_proj(("right", 0), 1)
         load_y(0)
+        quantize_proj(("right", 0), 0, 1)
+        turn_proj(("right", 0), 2, 3)
+        stage_proj(("right", 0), 2)
+        turn_proj(("right", 0), 3, 5)
         stage_proj(("right", 0), 3)
         load_prior((0, 0))
-        quantize_proj(("right", 0), 3, 4)
-        load_proj(("right", 2), 0, 2)
+        turn_proj(("left", 0), 0, 4)
         quantize_proj(("right", 0), 1, 2)
+        load_proj(("right", 2), 0, 2)
+        quantize_proj(("right", 0), 2, 3)
+        turn_proj(("left", 0), 1, 0)
+        turn_proj(("left", 0), 3, 3)
+        turn_proj(("left", 0), 2, 5)
+        quantize_proj(("right", 0), 3, 4)
         stage_proj(("left", 0), 0)
-        quantize_proj(("right", 0), 0, 1)
         stage_proj(("left", 0), 1)
-        quantize_proj(("left", 0), 0, 1)
-        turn_proj(("left", 0), 3, 0)
-        stage_proj(("left", 0), 2)
-        pair_matmul((0, 0), 0, 5)
-        quantize_proj(("left", 0), 2, 3)
         stage_proj(("left", 0), 3)
-        quantize_proj(("left", 0), 1, 2)
-        stage_y(0, 0, 2, on_scalar)
-        pair_matmul((0, 0), 1, 0)
-        pair_matmul((0, 0), 2, 1)
-        quantize_proj(("left", 0), 3, 4)
         load_near((0, 0), 0, 2)
-        pair_matmul((0, 0), 3, 4)
-        turn_proj(("right", 2), 0, 3)
+        quantize_proj(("left", 0), 0, 1)
+        stage_proj(("left", 0), 2)
+        quantize_proj(("left", 0), 1, 2)
+        pair_matmul((0, 0), 0, 0)
+        quantize_proj(("left", 0), 3, 4)
+        pair_matmul((0, 0), 1, 7)
         add_prior((0, 0), 0)
-        load_proj(("right", 2), 2, 4)
+        pair_matmul((0, 0), 3, 4)
+        quantize_proj(("left", 0), 2, 3)
         stage_y(0, 2, 4, on_scalar)
-        add_prior((0, 0), 1)
-        load_proj(("left", 1), 0, 2)
-        add_prior((0, 0), 2)
         turn_proj(("right", 2), 1, 2)
-        turn_proj(("right", 2), 2, 0)
-        stage_proj(("right", 2), 0)
-        turn_proj(("right", 2), 3, 1)
-        load_near((0, 0), 2, 4)
+        stage_y(0, 0, 2, on_scalar)
+        load_proj(("right", 2), 2, 4)
+        add_prior((0, 0), 1)
+        turn_proj(("right", 2), 0, 1)
+        pair_matmul((0, 0), 2, 6)
         stage_proj(("right", 2), 1)
-        load_y(1)
-        stage_proj(("right", 2), 2)
-        gate((0, 0), 0, 0, 4)
+        load_proj(("left", 1), 0, 2)
         add_prior((0, 0), 3)
-        quantize_y(0)
-        turn_pair((0, 0), 0, 6)
+        turn_proj(("right", 2), 3, 3)
+        stage_proj(("right", 2), 0)
+        gate((0, 0), 0, 0, 4)
+        add_prior((0, 0), 2)
+        load_proj(("left", 1), 2, 4)
+        load_near((0, 0), 2, 4)
         stage_proj(("right", 2), 3)
-        turn_proj(("left", 1), 1, 4)
-        quantize_proj(("right", 2), 0, 2)
-        stage_proj(("left", 1), 1)
-        turn_proj(("left", 1), 0, 3)
+        turn_proj(("right", 2), 2, 2)
+        turn_pair((0, 0), 0, 7)
+        turn_proj(("left", 1), 1, 5)
+        stage_proj(("right", 2), 2)
+        quantize_y(0)
+        turn_proj(("left", 1), 0, 0)
         quantize_proj(("right", 2), 2, 4)
-        pair_matmul((0, 2), 1, 1)
-        pair_matmul((0, 2), 3, 7)
-        stage_proj(("left", 1), 0)
-        pair_matmul((0, 2), 0, 3)
-        stage_along_m((0, 0), 0)
+        quantize_proj(("right", 2), 0, 2)
+        turn_proj(("left", 1), 3, 3)
         load_prior((0, 2))
         gate((0, 0), 1, 0, 4)
-        quantize_proj(("left", 1), 0, 2)
-        pair_matmul((0, 2), 2, 6)
-        load_proj(("left", 1), 2, 4)
-        turn_proj(("left", 1), 3, 0)
-        add_prior((0, 2), 1)
-        stage_along_i((0, 0), 0, 1, on_scalar)
         load_proj(("right", 1), 0, 4)
-        add_prior((0, 2), 3)
-        stage_y(1, 2, 4, on_scalar)
-        stage_along_i_gpsimd((0, 0), 1, 4)
-        add_prior((0, 2), 0)
-        add_prior((0, 2), 2)
-        quantize_along_i((0, 0), 0, 4)
-        gate((0, 2), 1, 0, 4)
+        stage_along_m((0, 0), 0)
+        load_y(1)
+        stage_proj(("left", 1), 1)
+        stage_along_i((0, 0), 0, 1, on_scalar)
         stage_proj(("left", 1), 3)
-        turn_proj(("left", 1), 2, 4)
-        load_near((1, 0))
-        stage_proj(("left", 1), 2)
-        turn_pair((0, 0), 1, 2)
-        pair_matmul((1, 0), 0, 5)
-        stage_along_m((0, 0), 1)
-        stage_y(1, 0, 2, on_scalar)
+        turn_proj(("left", 1), 2, 6)
+        pair_matmul((0, 2), 3, 4)
+        stage_along_i_gpsimd((0, 0), 1, 4)
         load_prior((1, 0))
-        quantize_proj(("left", 1), 2, 4)
-        turn_proj(("right", 1), 1, 6)
+        pair_matmul((0, 2), 0, 1)
+        pair_matmul((0, 2), 2, 2)
+        stage_proj(("left", 1), 2)
+        add_prior((0, 2), 3)
+        turn_pair((0, 0), 1, 3)
+        pair_matmul((0, 2), 1, 7)
+        stage_proj(("left", 1), 0)
+        add_prior((0, 2), 0)
+        turn_proj(("right", 1), 0, 5)
         load_proj(("right", 3), 0, 4)
-        turn_proj(("right", 1), 2, 7)
+        add_prior((0, 2), 2)
+        turn_proj(("right", 1), 1, 4)
+        quantize_proj(("left", 1), 0, 4)
+        stage_along_m((0, 0), 1)
+        add_prior((0, 2), 1)
+        turn_proj(("right", 1), 2, 3)
+        quantize_along_i((0, 0), 0, 4)
         gate((0, 2), 0, 0, 4)
-        turn_proj(("right", 1), 0, 3)
-        turn_proj(("right", 1), 3, 4)
-        stage_proj(("right", 1), 2)
-        stage_proj(("right", 1), 1)
-        pair_matmul((1, 0), 2, 2)
-        pair_matmul((1, 0), 1, 0)
-        quantize_along_m((0, 0), 0, 4)
-        add_prior((1, 0), 0)
-        add_prior((1, 0), 2)
-        stage_along_i_gpsimd((0, 2), 1, 4)
         stage_proj(("right", 1), 0)
-        pair_matmul((1, 0), 3, 7)
-        turn_pair((0, 2), 1, 6)
-        add_prior((1, 0), 1)
-        turn_pair((0, 2), 0, 1)
-        turn_proj(("right", 3), 3, 2)
-        add_prior((1, 0), 3)
-        load_v()
-        quantize_proj(("right", 1), 0, 2)
-        stage_along_i((0, 2), 0, 1, on_scalar)
+        pair_matmul((1, 0), 3, 1)
+        stage_y(1, 2, 4, on_scalar)
+        pair_matmul((1, 0), 0, 0)
+        gate((0, 2), 1, 0, 4)
+        pair_matmul((1, 0), 1, 6)
+        stage_proj(("right", 1), 2)
         load_prior((0, 1))
+        stage_proj(("right", 1), 1)
+        pair_matmul((1, 0), 2, 7)
+        add_prior((1, 0), 2)
+        load_near((1, 0))
+        stage_along_i((0, 2), 0, 1, on_scalar)
+        load_v()
+        turn_pair((0, 2), 0, 2)
+        stage_along_i_gpsimd((0, 2), 1, 4)
+        stage_y(1, 0, 2, on_scalar)
+        turn_proj(("right", 1), 3, 3)
         stage_proj(("right", 1), 3)
-        turn_proj(("right", 3), 0, 4)
-        quantize_proj(("right", 1), 2, 4)
-        gate((1, 0), 0, 0, 4)
-        gate((1, 0), 1, 0, 4)
-        quantize_y(1)
-        turn_proj(("right", 3), 1, 3)
-        pair_matmul((0, 1), 1, 5)
-        stage_along_m((0, 2), 1)
-        stage_proj(("right", 3), 0)
+        turn_pair((0, 2), 1, 5)
+        add_prior((1, 0), 1)
+        turn_proj(("right", 3), 1, 4)
         stage_proj(("right", 3), 1)
-        pair_matmul((0, 1), 2, 0)
-        load_prior((1, 3))
-        pair_matmul((0, 1), 0, 6)
-        turn_pair((1, 0), 0, 7)
-        stage_proj(("right", 3), 3)
-        add_prior((0, 1), 0)
-        add_prior((0, 1), 1)
-        stage_along_m((0, 2), 0)
-        turn_proj(("right", 3), 2, 3)
-        stage_along_i((1, 0), 0, 1, on_scalar)
-        load_near((0, 1))
-        stage_along_i_gpsimd((1, 0), 1, 4)
-        turn_pair((1, 0), 1, 2)
-        pair_matmul((0, 1), 3, 4)
-        load_near((1, 1))
-        stage_along_m((1, 0), 0)
-        load_prior((0, 3))
-        keep_busy(3, ("right", 0), 512, 1)
-        add_prior((0, 1), 2)
-        load_prior((1, 2))
-        pair_matmul((1, 2), 2, 7)
-        add_prior((0, 1), 3)
-        stage_proj(("right", 3), 2)
-        quantize_along_i((1, 0), 0, 4)
-        gate((0, 1), 0, 0, 4)
-        load_prior((1, 1))
-        gate((0, 1), 1, 0, 4)
-        quantize_proj(("right", 3), 0, 2)
+        add_prior((1, 0), 3)
+        turn_proj(("right", 3), 0, 7)
         pair_matmul((1, 2), 3, 6)
-        stage_along_m((1, 0), 1)
-        quantize_proj(("right", 3), 2, 4)
-        receptor_passes(0, 0, 5)
-        emit("rec", 0, 0, on_scalar)
-        receptor_passes(0, 2, 3)
-        receptor_passes(0, 3, 0)
-        quantize_along_i((0, 2), 0, 4)
-        quantize_along_m((0, 2), 0, 4)
-        turn_pair((0, 1), 0, 1)
-        emit("rec", 0, 2, on_scalar)
-        turn_pair((0, 1), 1, 2)
-        emit("rec", 0, 3, on_scalar)
-        receptor_passes(0, 1, 4)
-        pair_matmul((0, 3), 3, 3)
-        add_prior((0, 3), 3)
-        pair_matmul((0, 3), 0, 0)
+        stage_proj(("right", 3), 0)
+        turn_proj(("right", 3), 3, 1)
+        add_prior((1, 0), 0)
+        quantize_proj(("right", 1), 0, 4)
+        stage_along_m((0, 2), 1)
+        load_near((0, 1))
+        load_near((1, 1))
+        quantize_along_m((0, 0), 0, 4)
+        gate((1, 0), 0, 0, 4)
+        turn_proj(("right", 3), 2, 3)
+        load_prior((1, 2))
+        quantize_y(1)
+        stage_proj(("right", 3), 2)
+        pair_matmul((0, 1), 3, 4)
+        spill((0, 1), 3)
+        pair_matmul((0, 1), 0, 5)
+        gate((1, 0), 1, 0, 4)
+        load_prior((0, 3))
+        pair_matmul((0, 1), 1, 7)
+        keep_busy(3, ("right", 0), 512, 0)
+        stage_proj(("right", 3), 3)
+        spill((1, 2), 3)
+        quantize_proj(("right", 3), 0, 4)
+        pair_matmul((0, 1), 2, 4)
+        pair_matmul((1, 1), 1, 0)
+        turn_pair((1, 0), 1, 1)
+        stage_along_m((0, 2), 0)
+        add_prior((0, 1), 2)
+        turn_pair((1, 0), 0, 2)
+        add_prior((0, 1), 1)
+        stage_along_i((1, 0), 0, 4, on_scalar)
+        pair_matmul((0, 3), 2, 6)
+        add_prior((0, 1), 0)
+        add_prior_gpsimd((0, 1), 3)
+        quantize_along_i((1, 0), 0, 4)
+        pair_matmul((0, 3), 3, 4)
         pair_matmul((0, 3), 1, 5)
-        add_prior((0, 3), 0)
+        stage_along_m((1, 0), 0)
+        receptor_passes(0, 1, 7)
+        gate((0, 1), 0, 0, 4)
+        stage_along_m((1, 0), 1)
+        quantize_along_m((0, 2), 0, 4)
+        receptor_passes(0, 2, 3)
+        load_prior((1, 3))
+        spill((0, 3), 3)
+        gate((0, 1), 1, 0, 4)
         emit("rec", 0, 1, on_scalar)
-        pair_matmul((0, 3), 2, 4)
-        pair_matmul((1, 1), 3, 3)
-        stage_along_i_gpsimd((0, 1), 1, 4)
-        add_prior((0, 3), 1)
-        pair_matmul((1, 2), 1, 0)
-        stage_along_i((0, 1), 0, 1, on_scalar)
-        add_prior((1, 2), 2)
-        stage_along_m((0, 1), 1)
-        pair_matmul((1, 2), 0, 2)
-        gate((0, 3), 0, 0, 4)
+        receptor_passes(0, 0, 2)
+        quantize_along_i((0, 2), 0, 4)
+        pair_matmul((0, 3), 0, 1)
+        emit("rec", 0, 2, on_scalar)
+        turn_pair((0, 1), 0, 4)
+        emit("rec", 0, 0, on_scalar)
+        add_prior((0, 3), 0)
         add_prior((0, 3), 2)
-        quantize_along_m((1, 0), 0, 4)
-        turn_pair((0, 3), 0, 7)
         stage_along_m((0, 1), 0)
+        add_prior((0, 3), 1)
+        add_prior_gpsimd((0, 3), 3)
+        quantize_along_m((1, 0), 0, 4)
+        turn_pair((0, 1), 1, 3)
+        stage_along_m((0, 1), 1)
+        gate((0, 3), 0, 0, 4)
+        pair_matmul((1, 2), 0, 7)
+        load_prior((1, 1))
+        receptor_passes(0, 3, 6)
+        emit("rec", 0, 3, on_scalar)
         gate((0, 3), 1, 0, 4)
-        stage_along_m((0, 3), 0)
-        pair_matmul((1, 1), 2, 1)
+        pair_matmul((1, 2), 1, 4)
+        stage_along_i((0, 1), 0, 4, on_scalar)
+        pair_matmul((1, 2), 2, 1)
         quantize_along_m((0, 1), 0, 4)
-        pair_matmul((1, 3), 1, 5)
-        stage_along_i((0, 3), 0, 1, on_scalar)
-        turn_pair((0, 3), 1, 4)
+        turn_pair((0, 3), 0, 5)
+        pair_matmul((1, 1), 3, 3)
+        turn_pair((0, 3), 1, 2)
+        ligand_passes(0, 2, [0, 2, 1], True, False, 6)
+        stage_along_m((0, 3), 0)
+        add_prior((1, 2), 2)
+        add_prior_gpsimd((1, 2), 3)
+        ligand_passes(0, 1, [0, 2, 1], True, False, 5)
         stage_along_m((0, 3), 1)
-        add_prior((1, 1), 2)
-        stage_along_i_gpsimd((0, 3), 1, 4)
         add_prior((1, 2), 0)
-        ligand_passes(0, 1, [0, 2, 1], True, False, 7)
+        pair_matmul((1, 1), 2, 2)
+        stage_along_i((0, 3), 0, 4, on_scalar)
         pair_matmul((1, 1), 0, 1)
         add_prior((1, 2), 1)
-        add_prior((1, 2), 3)
-        ligand_passes(0, 2, [0, 2, 1], True, False, 4)
         quantize_along_m((0, 3), 0, 4)
-        ligand_passes(0, 0, [0, 2, 1], True, False, 2)
-        gate((1, 2), 0, 0, 4)
-        quantize_along_i((0, 1), 0, 4)
-        ligand_passes(0, 0, [3], False, True)
-        emit("lig", 0, 0, on_scalar)
-        ligand_passes(0, 2, [3], False, True)
-        emit("lig", 0, 2, on_scalar)
         ligand_passes(0, 1, [3], False, True)
-        ligand_passes(0, 3, [0, 2, 1, 3], True, True, 6)
+        gate((1, 2), 0, 0, 4)
+        ligand_passes(0, 2, [3], False, True)
+        spill((1, 1), 3)
         emit("lig", 0, 1, on_scalar)
-        emit("lig", 0, 3, on_scalar)
-        pair_matmul((1, 1), 1, 2)
         gate((1, 2), 1, 0, 4)
-        add_prior((1, 1), 0)
-        stage_along_i_gpsimd((1, 2), 1, 4)
-        turn_pair((1, 2), 0, 4)
-        add_prior((1, 1), 3)
-        add_prior((1, 3), 1)
-        turn_pair((1, 2), 1, 6)
-        pair_matmul((1, 3), 2, 0)
-        pair_matmul((1, 3), 0, 1)
-        stage_along_i((1, 2), 0, 1, on_scalar)
-        stage_along_m((1, 2), 1)
-        add_prior((1, 1), 1)
-        pair_matmul((1, 3), 3, 3)
-        gate((1, 1), 1, 2, 4)
-        quantize_along_i((1, 2), 0, 4)
-        receptor_passes(2, 0, 7)
-        gate((1, 1), 1, 0, 2)
-        receptor_passes(2, 3, 5)
+        emit("lig", 0, 2, on_scalar)
+        pair_matmul((1, 3), 1, 7)
+        turn_pair((1, 2), 0, 3)
+        quantize_along_i((0, 1), 0, 4)
         stage_along_m((1, 2), 0)
-        emit("rec", 2, 0, on_scalar)
-        receptor_passes(2, 2, 6)
+        ligand_passes(0, 0, [0, 2, 1], True, False, 4)
+        ligand_passes(0, 3, [0, 2, 1, 3], True, True, 6)
+        turn_pair((1, 2), 1, 3)
+        add_prior_gpsimd((1, 1), 3)
+        pair_matmul((1, 3), 2, 5)
+        add_prior((1, 3), 1)
+        stage_along_i((1, 2), 0, 4, on_scalar)
+        ligand_passes(0, 0, [3], False, True)
+        add_prior((1, 1), 1)
+        add_prior((1, 1), 0)
+        add_prior((1, 1), 2)
+        stage_along_m((1, 2), 1)
+        pair_matmul((1, 3), 0, 7)
+        quantize_along_i((1, 2), 0, 4)
+        emit("lig", 0, 0, on_scalar)
+        gate((1, 1), 1, 2, 4)
+        receptor_passes(2, 1, 3)
+        gate((1, 1), 1, 0, 2)
         gate((1, 1), 0, 0, 4)
-        emit("rec", 2, 3, on_scalar)
-        receptor_passes(2, 1, 7)
-        quantize_along_i((0, 3), 0, 4)
-        emit("rec", 2, 2, on_scalar)
-        add_prior((1, 3), 0)
+        emit("lig", 0, 3, on_scalar)
         emit("rec", 2, 1, on_scalar)
-        quantize_along_m((1, 2), 0, 4)
+        receptor_passes(2, 0, 2)
+        pair_matmul((1, 3), 3, 4)
+        quantize_along_i((0, 3), 0, 4)
+        emit("rec", 2, 0, on_scalar)
         add_prior((1, 3), 3)
-        add_prior((1, 3), 2)
+        quantize_along_m((1, 2), 0, 4)
+        receptor_passes(2, 3, 6)
+        emit("rec", 2, 3, on_scalar)
+        turn_pair((1, 1), 1, 0)
         stage_along_i((1, 1), 0, 2, on_scalar)
-        stage_along_i((1, 1), 2, 4, on_scalar)
-        turn_pair((1, 1), 0, 5)
-        turn_pair((1, 1), 1, 2)
-        quantize_along_i((1, 1), 0, 4)
-        gate((1, 3), 1, 0, 2)
+        add_prior((1, 3), 2)
+        turn_pair((1, 1), 0, 1)
+        receptor_passes(2, 2, 3)
         ligand_passes(1, 0, [0, 2], True, False, 6)
+        stage_along_i((1, 1), 2, 4, on_scalar)
+        emit("rec", 2, 2, on_scalar)
         stage_along_m((1, 1), 1)
-        gate((1, 3), 0, 0, 2)
-        ligand_passes(1, 1, [0, 2], True, False, 7)
-        ligand_passes(1, 3, [0, 2], True, False, 1)
-        receptor_passes(1, 3, 4)
         stage_along_m((1, 1), 0)
-        emit("rec", 1, 3, on_vector)
-        stage_along_i((1, 3), 0, 2, on_scalar)
+        add_prior((1, 3), 0)
+        ligand_passes(1, 1, [0, 2], True, False, 4)
+        quantize_along_i((1, 1), 0, 4)
+        gate((1, 3), 0, 0, 2)
+        gate((1, 3), 1, 0, 2)
+        receptor_passes(1, 3, 5)
+        receptor_passes(1, 0, 2)
         gate((1, 3), 1, 2, 4)
-        receptor_passes(1, 0, 3)
-        receptor_passes(1, 2, 0)
-        emit("rec", 1, 0, on_scalar)
-        gate((1, 3), 0, 2, 4)
-        receptor_passes(1, 1, 5)
-        turn_pair((1, 3), 1, 2)
-        quantize_along_i((1, 3), 0, 2)
-        turn_pair((1, 3), 0, 4)
-        emit("rec", 1, 1, on_scalar)
+        receptor_passes(1, 2, 7)
+        stage_along_i((1, 3), 0, 2, on_scalar)
+        emit("rec", 1, 0, on_vector)
+        receptor_passes(1, 1, 1)
         emit("rec", 1, 2, on_scalar)
-        stage_along_m((1, 3), 0)
-        stage_along_i((1, 3), 2, 4, on_vector)
-        receptor_passes(3, 1, 3)
+        ligand_passes(1, 3, [0, 2], True, False, 3)
+        gate((1, 3), 0, 2, 4)
+        emit("rec", 1, 1, on_scalar)
+        quantize_along_i((1, 3), 0, 2)
+        turn_pair((1, 3), 0, 0)
+        emit("rec", 1, 3, on_vector)
+        turn_pair((1, 3), 1, 2)
         quantize_along_m((1, 1), 0, 4)
-        receptor_passes(3, 0, 5)
-        ligand_passes(1, 2, [0, 2], True, False, 0)
-        emit("rec", 3, 1, on_vector)
-        quantize_along_i((1, 3), 2, 4)
-        receptor_passes(3, 2, 3)
-        ligand_passes(1, 1, [1], False, False)
-        emit("rec", 3, 0, on_scalar)
-        stage_along_m((1, 3), 1)
-        quantize_along_m((1, 3), 0, 2)
-        ligand_passes(1, 1, [3], False, True)
-        receptor_passes(3, 3, 5)
-        emit("rec", 3, 2, on_vector)
-        emit("lig", 1, 1, on_vector)
-        quantize_along_m((1, 3), 2, 4)
+        receptor_passes(3, 0, 1)
+        stage_along_i((1, 3), 2, 4, on_vector)
+        receptor_passes(3, 1, 7)
         ligand_passes(1, 0, [1], False, False)
+        ligand_passes(1, 1, [1], False, False)
+        stage_along_m((1, 3), 0)
+        quantize_along_m((1, 3), 0, 2)
+        quantize_along_i((1, 3), 2, 4)
+        emit("rec", 3, 0, on_scalar)
+        ligand_passes(1, 1, [3], False, True)
+        emit("rec", 3, 1, on_scalar)
+        stage_along_m((1, 3), 1)
+        receptor_passes(3, 3, 5)
+        emit("lig", 1, 1, on_vector)
+        emit("rec", 3, 3, on_vector)
+        receptor_passes(3, 2, 1)
+        emit("rec", 3, 2, on_scalar)
+        quantize_along_m((1, 3), 2, 4)
         ligand_passes(1, 0, [3], False, True)
-        emit("rec", 3, 3, on_scalar)
+        ligand_passes(1, 2, [0, 2], True, False, 7)
         ligand_passes(1, 2, [1], False, False)
-        emit("lig", 1, 0, on_vector)
         ligand_passes(1, 2, [3], False, True)
+        emit("lig", 1, 0, on_vector)
         emit("lig", 1, 2, on_vector)
         ligand_passes(1, 3, [1], False, False)
         ligand_passes(1, 3, [3], False, True)

@@ -108,8 +108,9 @@ def tile_pair_tensor_messages_s8_kernel(tc, left, right, prior, near, v_words, v
             if key not in staged:
                 staged[key] = ring.tile([P, K_PASSES * SPAN * PACK], BF16, name="staged", align_bytes=64)
             dst = staged[key][:].bitcast(F32)[:, span(place(key, quarter), SPAN)]
-            nc.scalar.copy(out=dst.rearrange("p (a r u) -> p a r u", a=2, u=2),
-                           in_=acc[key, quarter][:].rearrange("p (a u r) -> p a r u", a=2, u=2))
+            order = "p a r u" if key[0] == "left" else "p r a u"
+            nc.scalar.copy(out=dst.rearrange("p (%s) -> %s" % (order[2:], order), a=2, u=2),
+                           in_=acc[key, quarter][:].rearrange("p (a u r) -> " + order, a=2, u=2))
 
         def quantize_proj(key, lo, hi):
             quantize(key, staged[key], slice(2 * P * lo, 2 * P * hi), LIG if key[0] == "left" else REC)
@@ -128,9 +129,9 @@ def tile_pair_tensor_messages_s8_kernel(tc, left, right, prior, near, v_words, v
         def add_prior(b, t):
             if (b, t // 2) not in summed:
                 summed[b, t // 2] = ring.tile([P, 2, SPAN], F32, name="summed%d" % (t // 2), bufs=2 - t // 2)
-            nc.vector.tensor_tensor(out=summed[b, t // 2][:, t % 2, :].rearrange("p (s q) -> p s q", s=PACK),
-                                    in0=acc[b, t][:].rearrange("p (s q) -> p s q", s=PACK),
-                                    in1=prior_sb[b][:, t, :].rearrange("p (q s) -> p s q", s=PACK), op=ALU.add)
+            nc.vector.tensor_tensor(out=summed[b, t // 2][:, t % 2, :].rearrange("p (h q e) -> p h q e", h=2, e=2),
+                                    in0=acc[b, t][:].rearrange("p (h q e) -> p h q e", h=2, e=2),
+                                    in1=prior_sb[b][:, t, :].rearrange("p (q h e) -> p h q e", h=2, e=2), op=ALU.add)
 
         spilled = {}
 
@@ -141,38 +142,38 @@ def tile_pair_tensor_messages_s8_kernel(tc, left, right, prior, near, v_words, v
         def add_prior_gpsimd(b, t):
             if (b, t // 2) not in summed:
                 summed[b, t // 2] = ring.tile([P, 2, SPAN], F32, name="summed%d" % (t // 2), bufs=2 - t // 2)
-            nc.gpsimd.tensor_tensor(out=summed[b, t // 2][:, t % 2, :].rearrange("p (s q) -> p s q", s=PACK),
-                                    in0=spilled[b][:].rearrange("p (s q) -> p s q", s=PACK),
-                                    in1=prior_sb[b][:, t, :].rearrange("p (q s) -> p s q", s=PACK), op=ALU.add)
+            nc.gpsimd.tensor_tensor(out=summed[b, t // 2][:, t % 2, :].rearrange("p (h q e) -> p h q e", h=2, e=2),
+                                    in0=spilled[b][:].rearrange("p (h q e) -> p h q e", h=2, e=2),
+                                    in1=prior_sb[b][:, t, :].rearrange("p (q h e) -> p h q e", h=2, e=2), op=ALU.add)
 
-        def gate(b, u, lo, hi):
+        def gate(b, slots, h):
             if b not in paired:
-                paired[b] = ring.tile([P, 2, 2 * SPAN], BF16, name="paired", bufs=3)
-            for s in range(lo, hi):
+                paired[b] = ring.tile([P, PACK, SPAN], BF16, name="paired", bufs=3)
+            for t in slots:
                 nc.vector.scalar_tensor_tensor(
-                    out=paired[b][:, u, span(s, 2 * P)].rearrange("p (q e) -> p q e", e=2),
-                    in0=summed[b, u][:, :, span(s, P)].rearrange("p e q -> p q e"), scalar=0.0,
-                    in1=near_sb[b[0], b[1] % C][:, span(u, 2), s:SPAN:PACK].rearrange("p e q -> p q e"),
+                    out=paired[b][:, t, span(h, 2 * P)].rearrange("p (q e) -> p q e", e=2),
+                    in0=summed[b, t // 2][:, t % 2, span(h, 2 * P)].rearrange("p (q e) -> p q e", e=2), scalar=0.0,
+                    in1=near_sb[b[0], b[1] % C][:, t, :].rearrange("p (q h e) -> p h q e", h=2, e=2)[:, h, :, :],
                     op0=ALU.max, op1=ALU.mult)
 
         def turn_pair(b, u, n):
             acc[b, "turned", u] = bank(n)
             words = paired[b][:].bitcast(F32)
-            for s in range(PACK):
-                nc.tensor.transpose(acc[b, "turned", u][:, span(s, P)], words[:, u, span(s, P)], ident[:])
+            for a in range(2):
+                for h in range(2):
+                    nc.tensor.transpose(acc[b, "turned", u][:, span(2 * a + h, P)], words[:, 2 * u + a, span(h, P)], ident[:])
 
         def stage_along_m(b, u):
             if b not in along_m:
                 along_m[b] = ring.tile([P, SPAN * PACK], BF16, name="along_m", align_bytes=64)
-            nc.scalar.copy(out=along_m[b][:, span(u, 2 * SPAN)].rearrange("q (e p s) -> q e p s", e=2, s=PACK),
-                           in_=acc[b, "turned", u][:].bitcast(BF16).rearrange("q (s p e) -> q e p s", s=PACK, e=2))
+            nc.scalar.copy(out=along_m[b][:].bitcast(F32)[:, span(u, SPAN)].rearrange("q (a p h) -> q a p h", a=2, h=2),
+                           in_=acc[b, "turned", u][:].rearrange("q (a h p) -> q a p h", a=2, h=2))
 
-        def stage_along_i(b, lo, hi, copy):
+        def stage_along_i(b, h, lo, hi, copy):
             if b not in along_i:
                 along_i[b] = ring.tile([P, SPAN * PACK], BF16, name="along_i", align_bytes=64)
-            cols = slice(int(lo * P), int(hi * P))
-            copy(out=along_i[b][:].bitcast(F32).rearrange("p (c u) -> p c u", u=2)[:, cols, :],
-                 in_=paired[b][:].bitcast(F32).rearrange("p u c -> p c u")[:, cols, :])
+            copy(out=along_i[b][:, span(h, 2 * SPAN)].rearrange("p (e q t) -> p e q t", e=2, t=PACK)[:, lo:hi, :, :],
+                 in_=paired[b][:, :, span(h, 2 * P)].rearrange("p t (q e) -> p e q t", e=2)[:, lo:hi, :, :])
 
         def quantize_along_i(b, lo, hi):
             quantize(("zi", b), along_i[b], slice(lo * P, hi * P), ZI_BUFS)
@@ -210,322 +211,351 @@ def tile_pair_tensor_messages_s8_kernel(tc, left, right, prior, near, v_words, v
             for g in range(LIG):
                 mx(acc["rec", n, s], ("zi", (g, n)), span(s, P), ("y", g), slice(0, R), g == 0, g == LIG - 1)
 
+        res = {}
+
         def emit(kind, n, slot, copy):
-            res = ring.tile([P, R], F32, name="res", bufs=8)
-            copy(out=res[:], in_=acc[kind, n, slot][:])
-            nc.sync.dma_start(out=rows(out_0 if kind == "lig" else out_1, n)[:, slot, :], in_=res[:])
+            key = (kind, n, slot // 2)
+            if key not in res:
+                res[key] = ring.tile([P, 2, R], F32, name="res", bufs=4)
+            copy(out=res[key][:, slot % 2, :], in_=acc[kind, n, slot][:])
+
+        def store(kind, n, half):
+            nc.sync.dma_start(out=rows(out_0 if kind == "lig" else out_1, n)[:, span(half, 2), :], in_=res[kind, n, half][:])
 
         on_scalar, on_vector = nc.scalar.copy, nc.vector.tensor_copy
 
         def on_gpsimd(out, in_):
             nc.gpsimd.tensor_scalar(out=out, in0=in_, scalar1=1.0, scalar2=0.0, op0=ALU.mult, op1=ALU.add)
 
-        def stage_along_i_gpsimd(b, lo, hi):
-            if b not in along_i:
-                along_i[b] = ring.tile([P, SPAN * PACK], BF16, name="along_i", align_bytes=64)
-            cols = slice(int(lo * P), int(hi * P))
-            on_gpsimd(along_i[b][:].rearrange("p (c u e) -> p c u e", u=2, e=2)[:, cols, :, :],
-                      paired[b][:].rearrange("p u (c e) -> p c u e", e=2)[:, cols, :, :])
-
         load_proj(("right", 0), 0, 2)
+        turn_proj(("right", 0), 0, 2)
         load_proj(("right", 0), 2, 4)
-        turn_proj(("right", 0), 0, 0)
-        load_proj(("left", 0), 0, 2)
-        load_proj(("left", 0), 2, 4)
+        turn_proj(("right", 0), 1, 5)
+        turn_proj(("right", 0), 2, 7)
+        turn_proj(("right", 0), 3, 0)
         stage_proj(("right", 0), 0)
-        turn_proj(("right", 0), 1, 7)
-        stage_proj(("right", 0), 1)
-        load_y(0)
-        quantize_proj(("right", 0), 0, 1)
-        turn_proj(("right", 0), 2, 3)
-        stage_proj(("right", 0), 2)
-        turn_proj(("right", 0), 3, 5)
         stage_proj(("right", 0), 3)
+        load_proj(("left", 0), 2, 4)
+        turn_proj(("left", 0), 2, 4)
+        quantize_proj(("right", 0), 0, 1)
+        stage_proj(("right", 0), 2)
+        load_proj(("left", 0), 0, 2)
+        stage_proj(("right", 0), 1)
+        stage_proj(("left", 0), 2)
         load_prior((0, 0))
-        turn_proj(("left", 0), 0, 4)
+        keep_busy(2, ("right", 0), 256, 2)
+        load_y(0)
+        load_proj(("right", 2), 2, 4)
         quantize_proj(("right", 0), 1, 2)
         load_proj(("right", 2), 0, 2)
+        keep_busy(3, ("right", 0), 256, 0)
+        turn_proj(("left", 0), 0, 5)
         quantize_proj(("right", 0), 2, 3)
-        turn_proj(("left", 0), 1, 0)
-        turn_proj(("left", 0), 3, 3)
-        turn_proj(("left", 0), 2, 5)
+        turn_proj(("left", 0), 1, 6)
         quantize_proj(("right", 0), 3, 4)
+        quantize_proj(("left", 0), 2, 3)
         stage_proj(("left", 0), 0)
         stage_proj(("left", 0), 1)
-        stage_proj(("left", 0), 3)
-        load_near((0, 0), 0, 2)
+        turn_proj(("left", 0), 3, 1)
         quantize_proj(("left", 0), 0, 1)
-        stage_proj(("left", 0), 2)
+        pair_matmul((0, 0), 2, 3)
+        stage_proj(("left", 0), 3)
         quantize_proj(("left", 0), 1, 2)
         pair_matmul((0, 0), 0, 0)
-        quantize_proj(("left", 0), 3, 4)
-        pair_matmul((0, 0), 1, 7)
-        add_prior((0, 0), 0)
-        pair_matmul((0, 0), 3, 4)
-        quantize_proj(("left", 0), 2, 3)
-        stage_y(0, 2, 4, on_scalar)
-        turn_proj(("right", 2), 1, 2)
-        stage_y(0, 0, 2, on_scalar)
-        load_proj(("right", 2), 2, 4)
-        add_prior((0, 0), 1)
-        turn_proj(("right", 2), 0, 1)
-        pair_matmul((0, 0), 2, 6)
-        stage_proj(("right", 2), 1)
-        load_proj(("left", 1), 0, 2)
-        add_prior((0, 0), 3)
-        turn_proj(("right", 2), 3, 3)
-        stage_proj(("right", 2), 0)
-        gate((0, 0), 0, 0, 4)
         add_prior((0, 0), 2)
+        load_near((0, 0), 0, 2)
+        quantize_proj(("left", 0), 3, 4)
+        pair_matmul((0, 0), 1, 4)
+        add_prior((0, 0), 0)
+        turn_proj(("right", 2), 2, 1)
+        stage_y(0, 0, 2, on_scalar)
+        turn_proj(("right", 2), 0, 2)
+        load_proj(("left", 1), 0, 2)
+        add_prior((0, 0), 1)
         load_proj(("left", 1), 2, 4)
+        turn_proj(("right", 2), 1, 5)
+        turn_proj(("right", 2), 3, 3)
+        stage_y(0, 2, 4, on_scalar)
+        stage_proj(("right", 2), 0)
+        stage_proj(("right", 2), 2)
         load_near((0, 0), 2, 4)
         stage_proj(("right", 2), 3)
-        turn_proj(("right", 2), 2, 2)
-        turn_pair((0, 0), 0, 7)
-        turn_proj(("left", 1), 1, 5)
-        stage_proj(("right", 2), 2)
+        gate((0, 0), [0, 1], 0)
+        pair_matmul((0, 0), 3, 4)
+        turn_proj(("left", 1), 0, 2)
+        gate((0, 0), [0, 1], 1)
         quantize_y(0)
-        turn_proj(("left", 1), 0, 0)
-        quantize_proj(("right", 2), 2, 4)
-        quantize_proj(("right", 2), 0, 2)
-        turn_proj(("left", 1), 3, 3)
         load_prior((0, 2))
-        gate((0, 0), 1, 0, 4)
+        turn_proj(("left", 1), 1, 1)
+        turn_proj(("left", 1), 2, 3)
+        quantize_proj(("right", 2), 0, 2)
         load_proj(("right", 1), 0, 4)
-        stage_along_m((0, 0), 0)
-        load_y(1)
-        stage_proj(("left", 1), 1)
-        stage_along_i((0, 0), 0, 1, on_scalar)
-        stage_proj(("left", 1), 3)
-        turn_proj(("left", 1), 2, 6)
-        pair_matmul((0, 2), 3, 4)
-        stage_along_i_gpsimd((0, 0), 1, 4)
-        load_prior((1, 0))
-        pair_matmul((0, 2), 0, 1)
-        pair_matmul((0, 2), 2, 2)
-        stage_proj(("left", 1), 2)
-        add_prior((0, 2), 3)
-        turn_pair((0, 0), 1, 3)
-        pair_matmul((0, 2), 1, 7)
+        add_prior((0, 0), 3)
+        stage_proj(("right", 2), 1)
         stage_proj(("left", 1), 0)
-        add_prior((0, 2), 0)
-        turn_proj(("right", 1), 0, 5)
-        load_proj(("right", 3), 0, 4)
+        quantize_proj(("right", 2), 2, 4)
+        gate((0, 0), [2, 3], 1)
+        load_y(1)
+        pair_matmul((0, 2), 2, 7)
+        stage_proj(("left", 1), 2)
+        pair_matmul((0, 2), 0, 0)
+        load_prior((1, 0))
+        stage_proj(("left", 1), 1)
+        gate((0, 0), [2, 3], 0)
+        pair_matmul((0, 2), 3, 4)
         add_prior((0, 2), 2)
-        turn_proj(("right", 1), 1, 4)
-        quantize_proj(("left", 1), 0, 4)
+        stage_along_i((0, 0), 1, 0, 2, on_gpsimd)
+        add_prior((0, 2), 0)
+        turn_proj(("left", 1), 3, 5)
+        turn_pair((0, 0), 0, 0)
+        add_prior((0, 2), 3)
+        turn_pair((0, 0), 1, 1)
+        stage_along_i((0, 0), 0, 0, 2, on_scalar)
+        pair_matmul((0, 2), 1, 3)
+        turn_proj(("right", 1), 3, 7)
+        stage_proj(("left", 1), 3)
         stage_along_m((0, 0), 1)
+        gate((0, 2), [2, 3], 0)
+        gate((0, 2), [2, 3], 1)
+        stage_along_m((0, 0), 0)
+        load_proj(("right", 3), 0, 4)
+        turn_proj(("right", 1), 0, 5)
+        quantize_proj(("left", 1), 0, 4)
         add_prior((0, 2), 1)
-        turn_proj(("right", 1), 2, 3)
-        quantize_along_i((0, 0), 0, 4)
-        gate((0, 2), 0, 0, 4)
-        stage_proj(("right", 1), 0)
-        pair_matmul((1, 0), 3, 1)
+        turn_proj(("right", 1), 1, 4)
+        gate((0, 2), [0, 1], 1)
+        pair_matmul((1, 0), 0, 6)
         stage_y(1, 2, 4, on_scalar)
-        pair_matmul((1, 0), 0, 0)
-        gate((0, 2), 1, 0, 4)
-        pair_matmul((1, 0), 1, 6)
-        stage_proj(("right", 1), 2)
-        load_prior((0, 1))
-        stage_proj(("right", 1), 1)
-        pair_matmul((1, 0), 2, 7)
-        add_prior((1, 0), 2)
-        load_near((1, 0))
-        stage_along_i((0, 2), 0, 1, on_scalar)
-        load_v()
-        turn_pair((0, 2), 0, 2)
-        stage_along_i_gpsimd((0, 2), 1, 4)
-        stage_y(1, 0, 2, on_scalar)
-        turn_proj(("right", 1), 3, 3)
         stage_proj(("right", 1), 3)
-        turn_pair((0, 2), 1, 5)
-        add_prior((1, 0), 1)
-        turn_proj(("right", 3), 1, 4)
-        stage_proj(("right", 3), 1)
-        add_prior((1, 0), 3)
-        turn_proj(("right", 3), 0, 7)
-        pair_matmul((1, 2), 3, 6)
-        stage_proj(("right", 3), 0)
-        turn_proj(("right", 3), 3, 1)
-        add_prior((1, 0), 0)
-        quantize_proj(("right", 1), 0, 4)
-        stage_along_m((0, 2), 1)
-        load_near((0, 1))
-        load_near((1, 1))
+        pair_matmul((1, 0), 3, 3)
+        stage_proj(("right", 1), 0)
+        pair_matmul((1, 0), 2, 2)
+        turn_proj(("right", 1), 2, 0)
+        load_near((1, 0))
+        stage_proj(("right", 1), 1)
+        pair_matmul((1, 0), 1, 5)
         quantize_along_m((0, 0), 0, 4)
-        gate((1, 0), 0, 0, 4)
-        turn_proj(("right", 3), 2, 3)
-        load_prior((1, 2))
-        quantize_y(1)
+        turn_proj(("right", 3), 2, 4)
+        gate((0, 2), [0, 1], 0)
+        stage_proj(("right", 1), 2)
+        quantize_along_i((0, 0), 0, 4)
+        stage_along_i((0, 2), 1, 0, 2, on_gpsimd)
+        turn_proj(("right", 3), 3, 7)
+        add_prior((1, 0), 2)
+        stage_y(1, 0, 2, on_scalar)
+        add_prior((1, 0), 3)
+        add_prior((1, 0), 0)
+        turn_proj(("right", 3), 1, 6)
+        quantize_proj(("right", 1), 0, 4)
+        add_prior((1, 0), 1)
         stage_proj(("right", 3), 2)
-        pair_matmul((0, 1), 3, 4)
-        spill((0, 1), 3)
-        pair_matmul((0, 1), 0, 5)
-        gate((1, 0), 1, 0, 4)
-        load_prior((0, 3))
-        pair_matmul((0, 1), 1, 7)
-        keep_busy(3, ("right", 0), 512, 0)
+        gate((1, 0), [0, 1], 0)
+        pair_matmul((0, 1), 3, 3)
         stage_proj(("right", 3), 3)
-        spill((1, 2), 3)
+        gate((1, 0), [2, 3], 0)
+        load_prior((0, 1))
+        stage_proj(("right", 3), 1)
+        spill((0, 1), 3)
+        turn_proj(("right", 3), 0, 1)
+        turn_pair((0, 2), 1, 2)
+        turn_pair((0, 2), 0, 6)
+        gate((1, 0), [0, 1], 1)
+        stage_proj(("right", 3), 0)
+        pair_matmul((0, 1), 0, 0)
+        gate((1, 0), [2, 3], 1)
         quantize_proj(("right", 3), 0, 4)
-        pair_matmul((0, 1), 2, 4)
-        pair_matmul((1, 1), 1, 0)
-        turn_pair((1, 0), 1, 1)
+        stage_along_m((0, 2), 1)
+        pair_matmul((0, 1), 1, 5)
         stage_along_m((0, 2), 0)
-        add_prior((0, 1), 2)
-        turn_pair((1, 0), 0, 2)
+        stage_along_i((1, 0), 1, 0, 2, on_scalar)
+        pair_matmul((0, 1), 2, 4)
+        turn_pair((1, 0), 1, 1)
+        pair_matmul((0, 3), 2, 2)
+        stage_along_i((0, 2), 0, 0, 2, on_scalar)
+        load_v()
         add_prior((0, 1), 1)
-        stage_along_i((1, 0), 0, 4, on_scalar)
-        pair_matmul((0, 3), 2, 6)
         add_prior((0, 1), 0)
+        add_prior((0, 1), 2)
+        pair_matmul((1, 2), 3, 6)
         add_prior_gpsimd((0, 1), 3)
-        quantize_along_i((1, 0), 0, 4)
-        pair_matmul((0, 3), 3, 4)
-        pair_matmul((0, 3), 1, 5)
-        stage_along_m((1, 0), 0)
-        receptor_passes(0, 1, 7)
-        gate((0, 1), 0, 0, 4)
-        stage_along_m((1, 0), 1)
-        quantize_along_m((0, 2), 0, 4)
-        receptor_passes(0, 2, 3)
+        load_near((0, 1))
+        quantize_y(1)
+        gate((0, 1), [2, 3], 1)
+        pair_matmul((1, 1), 1, 5)
+        stage_along_i((1, 0), 0, 0, 2, on_scalar)
+        load_prior((1, 1))
+        load_prior((0, 3))
         load_prior((1, 3))
-        spill((0, 3), 3)
-        gate((0, 1), 1, 0, 4)
-        emit("rec", 0, 1, on_scalar)
-        receptor_passes(0, 0, 2)
-        quantize_along_i((0, 2), 0, 4)
-        pair_matmul((0, 3), 0, 1)
-        emit("rec", 0, 2, on_scalar)
+        gate((0, 1), [0, 1], 0)
+        pair_matmul((0, 3), 3, 3)
+        load_near((1, 1))
+        gate((0, 1), [0, 1], 1)
+        pair_matmul((0, 3), 0, 7)
+        stage_along_m((1, 0), 1)
         turn_pair((0, 1), 0, 4)
-        emit("rec", 0, 0, on_scalar)
+        pair_matmul((0, 3), 1, 0)
+        quantize_along_i((1, 0), 0, 4)
+        load_prior((1, 2))
+        spill((1, 2), 3)
+        quantize_along_m((0, 2), 0, 4)
+        gate((0, 1), [2, 3], 0)
+        receptor_passes(0, 1, 1)
+        add_prior((0, 3), 1)
+        spill((0, 3), 3)
         add_prior((0, 3), 0)
+        turn_pair((0, 1), 1, 6)
         add_prior((0, 3), 2)
         stage_along_m((0, 1), 0)
-        add_prior((0, 3), 1)
-        add_prior_gpsimd((0, 3), 3)
-        quantize_along_m((1, 0), 0, 4)
-        turn_pair((0, 1), 1, 3)
-        stage_along_m((0, 1), 1)
-        gate((0, 3), 0, 0, 4)
+        turn_pair((1, 0), 0, 4)
+        receptor_passes(0, 2, 3)
         pair_matmul((1, 2), 0, 7)
-        load_prior((1, 1))
-        receptor_passes(0, 3, 6)
+        add_prior((1, 1), 1)
+        add_prior_gpsimd((0, 3), 3)
+        receptor_passes(0, 3, 2)
+        gate((0, 3), [2, 3], 0)
+        gate((0, 3), [0, 1], 0)
+        emit("rec", 0, 1, on_scalar)
+        stage_along_m((0, 1), 1)
+        receptor_passes(0, 0, 1)
+        emit("rec", 0, 2, on_scalar)
+        stage_along_m((1, 0), 0)
         emit("rec", 0, 3, on_scalar)
-        gate((0, 3), 1, 0, 4)
-        pair_matmul((1, 2), 1, 4)
-        stage_along_i((0, 1), 0, 4, on_scalar)
-        pair_matmul((1, 2), 2, 1)
-        quantize_along_m((0, 1), 0, 4)
-        turn_pair((0, 3), 0, 5)
-        pair_matmul((1, 1), 3, 3)
-        turn_pair((0, 3), 1, 2)
-        ligand_passes(0, 2, [0, 2, 1], True, False, 6)
-        stage_along_m((0, 3), 0)
+        pair_matmul((1, 1), 2, 6)
+        emit("rec", 0, 0, on_scalar)
+        gate((0, 3), [0, 1], 1)
+        quantize_along_i((0, 2), 0, 4)
+        pair_matmul((1, 2), 1, 3)
+        gate((0, 3), [2, 3], 1)
+        quantize_along_m((1, 0), 0, 4)
+        pair_matmul((1, 2), 2, 0)
+        stage_along_i((0, 1), 1, 0, 2, on_scalar)
         add_prior((1, 2), 2)
-        add_prior_gpsimd((1, 2), 3)
-        ligand_passes(0, 1, [0, 2, 1], True, False, 5)
+        add_prior((1, 2), 1)
+        turn_pair((0, 3), 1, 5)
+        turn_pair((0, 3), 0, 2)
         stage_along_m((0, 3), 1)
         add_prior((1, 2), 0)
-        pair_matmul((1, 1), 2, 2)
-        stage_along_i((0, 3), 0, 4, on_scalar)
-        pair_matmul((1, 1), 0, 1)
-        add_prior((1, 2), 1)
-        quantize_along_m((0, 3), 0, 4)
-        ligand_passes(0, 1, [3], False, True)
-        gate((1, 2), 0, 0, 4)
-        ligand_passes(0, 2, [3], False, True)
-        spill((1, 1), 3)
-        emit("lig", 0, 1, on_scalar)
-        gate((1, 2), 1, 0, 4)
-        emit("lig", 0, 2, on_scalar)
-        pair_matmul((1, 3), 1, 7)
-        turn_pair((1, 2), 0, 3)
+        stage_along_m((0, 3), 0)
+        pair_matmul((1, 3), 0, 4)
+        add_prior_gpsimd((1, 2), 3)
+        quantize_along_m((0, 1), 0, 4)
+        gate((1, 2), [0, 1], 0)
+        gate((1, 2), [2, 3], 0)
+        gate((1, 2), [0, 1], 1)
+        stage_along_i((0, 3), 0, 0, 2, on_scalar)
+        store("rec", 0, 1)
+        stage_along_i((0, 1), 0, 0, 2, on_scalar)
+        pair_matmul((1, 1), 3, 1)
+        gate((1, 2), [2, 3], 1)
+        pair_matmul((1, 1), 0, 5)
+        ligand_passes(0, 0, [0, 2, 1], True, False, 0)
         quantize_along_i((0, 1), 0, 4)
-        stage_along_m((1, 2), 0)
-        ligand_passes(0, 0, [0, 2, 1], True, False, 4)
-        ligand_passes(0, 3, [0, 2, 1, 3], True, True, 6)
-        turn_pair((1, 2), 1, 3)
-        add_prior_gpsimd((1, 1), 3)
-        pair_matmul((1, 3), 2, 5)
-        add_prior((1, 3), 1)
-        stage_along_i((1, 2), 0, 4, on_scalar)
-        ligand_passes(0, 0, [3], False, True)
-        add_prior((1, 1), 1)
+        quantize_along_m((0, 3), 0, 4)
+        stage_along_i((0, 3), 1, 0, 2, on_scalar)
+        ligand_passes(0, 2, [0, 2, 1], True, False, 7)
         add_prior((1, 1), 0)
+        add_prior((1, 1), 3)
+        ligand_passes(0, 1, [0, 2, 1], True, False, 3)
+        ligand_passes(0, 3, [0, 2, 1, 3], True, True, 2)
         add_prior((1, 1), 2)
-        stage_along_m((1, 2), 1)
-        pair_matmul((1, 3), 0, 7)
+        stage_along_i((1, 2), 1, 0, 2, on_gpsimd)
+        ligand_passes(0, 2, [3], False, True)
+        stage_along_i((1, 2), 0, 0, 2, on_scalar)
+        gate((1, 1), [0, 1], 0)
+        emit("lig", 0, 2, on_scalar)
+        turn_pair((1, 2), 0, 5)
         quantize_along_i((1, 2), 0, 4)
-        emit("lig", 0, 0, on_scalar)
-        gate((1, 1), 1, 2, 4)
-        receptor_passes(2, 1, 3)
-        gate((1, 1), 1, 0, 2)
-        gate((1, 1), 0, 0, 4)
+        turn_pair((1, 2), 1, 1)
         emit("lig", 0, 3, on_scalar)
-        emit("rec", 2, 1, on_scalar)
-        receptor_passes(2, 0, 2)
-        pair_matmul((1, 3), 3, 4)
+        gate((1, 1), [0, 1], 1)
+        stage_along_m((1, 2), 0)
+        ligand_passes(0, 0, [3], False, True)
+        store("rec", 0, 0)
+        gate((1, 1), [2, 3], 0)
+        pair_matmul((1, 3), 1, 7)
         quantize_along_i((0, 3), 0, 4)
-        emit("rec", 2, 0, on_scalar)
-        add_prior((1, 3), 3)
-        quantize_along_m((1, 2), 0, 4)
-        receptor_passes(2, 3, 6)
-        emit("rec", 2, 3, on_scalar)
-        turn_pair((1, 1), 1, 0)
-        stage_along_i((1, 1), 0, 2, on_scalar)
-        add_prior((1, 3), 2)
-        turn_pair((1, 1), 0, 1)
-        receptor_passes(2, 2, 3)
-        ligand_passes(1, 0, [0, 2], True, False, 6)
-        stage_along_i((1, 1), 2, 4, on_scalar)
-        emit("rec", 2, 2, on_scalar)
-        stage_along_m((1, 1), 1)
-        stage_along_m((1, 1), 0)
+        stage_along_m((1, 2), 1)
+        gate((1, 1), [2, 3], 1)
+        pair_matmul((1, 3), 2, 2)
+        stage_along_i((1, 1), 1, 0, 2, on_gpsimd)
+        emit("lig", 0, 0, on_scalar)
+        receptor_passes(2, 1, 5)
+        ligand_passes(0, 1, [3], False, True)
+        pair_matmul((1, 3), 3, 1)
+        emit("rec", 2, 1, on_scalar)
+        turn_pair((1, 1), 0, 0)
+        turn_pair((1, 1), 1, 5)
+        store("lig", 0, 1)
         add_prior((1, 3), 0)
-        ligand_passes(1, 1, [0, 2], True, False, 4)
+        add_prior((1, 3), 3)
+        emit("lig", 0, 1, on_scalar)
+        stage_along_i((1, 1), 0, 0, 2, on_scalar)
+        add_prior((1, 3), 2)
+        receptor_passes(2, 3, 6)
         quantize_along_i((1, 1), 0, 4)
-        gate((1, 3), 0, 0, 2)
-        gate((1, 3), 1, 0, 2)
-        receptor_passes(1, 3, 5)
-        receptor_passes(1, 0, 2)
-        gate((1, 3), 1, 2, 4)
-        receptor_passes(1, 2, 7)
-        stage_along_i((1, 3), 0, 2, on_scalar)
-        emit("rec", 1, 0, on_vector)
-        receptor_passes(1, 1, 1)
-        emit("rec", 1, 2, on_scalar)
-        ligand_passes(1, 3, [0, 2], True, False, 3)
-        gate((1, 3), 0, 2, 4)
-        emit("rec", 1, 1, on_scalar)
-        quantize_along_i((1, 3), 0, 2)
-        turn_pair((1, 3), 0, 0)
-        emit("rec", 1, 3, on_vector)
-        turn_pair((1, 3), 1, 2)
+        gate((1, 3), [2, 3], 0)
+        receptor_passes(2, 2, 4)
+        store("lig", 0, 0)
+        emit("rec", 2, 3, on_scalar)
+        receptor_passes(2, 0, 3)
+        receptor_passes(1, 1, 6)
+        stage_along_m((1, 1), 0)
+        receptor_passes(1, 2, 0)
+        add_prior((1, 3), 1)
+        receptor_passes(1, 3, 1)
+        stage_along_m((1, 1), 1)
+        emit("rec", 2, 0, on_scalar)
+        gate((1, 3), [0, 1], 0)
+        emit("rec", 2, 2, on_scalar)
+        quantize_along_m((1, 2), 0, 4)
+        receptor_passes(1, 0, 7)
         quantize_along_m((1, 1), 0, 4)
-        receptor_passes(3, 0, 1)
-        stage_along_i((1, 3), 2, 4, on_vector)
-        receptor_passes(3, 1, 7)
+        stage_along_i((1, 3), 0, 0, 2, on_scalar)
+        emit("rec", 1, 2, on_vector)
+        ligand_passes(1, 0, [0, 2], True, False, 3)
+        emit("rec", 1, 3, on_scalar)
+        ligand_passes(1, 3, [0, 2], True, False, 5)
+        store("rec", 2, 0)
+        quantize_along_i((1, 3), 0, 2)
+        gate((1, 3), [0, 1], 1)
         ligand_passes(1, 0, [1], False, False)
-        ligand_passes(1, 1, [1], False, False)
+        store("rec", 2, 1)
+        emit("rec", 1, 0, on_scalar)
+        ligand_passes(1, 3, [1], False, False)
+        receptor_passes(3, 0, 0)
+        turn_pair((1, 3), 0, 2)
+        store("rec", 1, 1)
+        gate((1, 3), [2, 3], 1)
+        emit("rec", 1, 1, on_scalar)
         stage_along_m((1, 3), 0)
+        stage_along_i((1, 3), 1, 0, 1, on_vector)
+        stage_along_i((1, 3), 1, 1, 2, on_vector)
+        turn_pair((1, 3), 1, 1)
+        store("rec", 1, 0)
         quantize_along_m((1, 3), 0, 2)
-        quantize_along_i((1, 3), 2, 4)
+        receptor_passes(3, 1, 7)
+        emit("rec", 3, 1, on_vector)
         emit("rec", 3, 0, on_scalar)
-        ligand_passes(1, 1, [3], False, True)
-        emit("rec", 3, 1, on_scalar)
         stage_along_m((1, 3), 1)
-        receptor_passes(3, 3, 5)
-        emit("lig", 1, 1, on_vector)
-        emit("rec", 3, 3, on_vector)
+        ligand_passes(1, 1, [0, 2], True, False, 4)
+        ligand_passes(1, 1, [1], False, False)
+        quantize_along_i((1, 3), 2, 4)
+        ligand_passes(1, 1, [3], False, True)
+        ligand_passes(1, 0, [3], False, True)
+        emit("lig", 1, 1, on_scalar)
+        store("rec", 3, 0)
         receptor_passes(3, 2, 1)
+        receptor_passes(3, 3, 2)
         emit("rec", 3, 2, on_scalar)
         quantize_along_m((1, 3), 2, 4)
-        ligand_passes(1, 0, [3], False, True)
-        ligand_passes(1, 2, [0, 2], True, False, 7)
+        ligand_passes(1, 3, [3], False, True)
+        emit("rec", 3, 3, on_scalar)
+        ligand_passes(1, 2, [0, 2], True, False, 0)
+        emit("lig", 1, 0, on_vector)
+        emit("lig", 1, 3, on_scalar)
+        store("lig", 1, 0)
         ligand_passes(1, 2, [1], False, False)
         ligand_passes(1, 2, [3], False, True)
-        emit("lig", 1, 0, on_vector)
-        emit("lig", 1, 2, on_vector)
-        ligand_passes(1, 3, [1], False, False)
-        ligand_passes(1, 3, [3], False, True)
-        emit("lig", 1, 3, on_scalar)
+        store("rec", 3, 1)
+        emit("lig", 1, 2, on_scalar)
+        store("lig", 1, 1)

from contextlib import ExitStack

import concourse.mybir as mybir
from concourse.masks import make_identity

F32 = mybir.dt.float32
BF16 = mybir.dt.bfloat16
I32 = mybir.dt.int32
U32 = mybir.dt.uint32
U8 = mybir.dt.uint8
FP8X4 = mybir.dt.float8_e4m3fn_x4
FP4X4 = mybir.dt.float4_e2m1fn_x4
ALU = mybir.AluOpType

I, J, C, K, R = 1024, 1024, 2, 1024, 512
M = C * J
P = 128
PACK = 4
SPAN = P * PACK
K_PASSES = K // SPAN
LIG = I // SPAN
REC = M // SPAN
FLOPS = 2 * I * M * K + 2 * I * M * R + 2 * M * I * R

ZI_BUFS, ZM_BUFS = 5, 6


def tile_pair_tensor_messages_s8_kernel(tc, left, right, prior, near, v_words, v_scales, y, out_0, out_1):
    nc = tc.nc
    with ExitStack() as ctx:
        keep = ctx.enter_context(tc.tile_pool(name="keep", bufs=1))
        ring = ctx.enter_context(tc.tile_pool(name="ring", bufs=2))
        psum = ctx.enter_context(tc.psum_pool(name="psum", bufs=1))
        ctx.enter_context(tc.manual_schedule())

        def bank(n):
            return psum.tile([P, SPAN], F32, name="bank%d" % n)

        ident = keep.tile([P, P], F32, name="ident")
        make_identity(nc, ident[:])
        v_codes = keep.tile([P, REC, 2 * R], U8, name="v_codes", align_bytes=64)
        v_plane = keep.tile([P, REC, R], U8, name="v_plane", align_bytes=64)
        nc.vector.memset(v_plane[:].bitcast(I32), 0)

        raw, staged, codes, scales, acc = {}, {}, {}, {}, {}
        prior_sb, near_sb, y_raw, y_staged = {}, {}, {}, {}
        summed, paired, along_i, along_m = {}, {}, {}, {}

        def rows(src, n):
            return src[n * SPAN:(n + 1) * SPAN, :].rearrange("(p t) d -> p t d", t=PACK)

        def span(n, width):
            return slice(n * width, (n + 1) * width)

        def load_proj(key, lo, hi):
            if key not in raw:
                raw[key] = ring.tile([P, PACK, K], BF16, name="raw", bufs=4)
            src = left if key[0] == "left" else right
            nc.sync.dma_start(out=raw[key][:, lo:hi, :], in_=rows(src, key[1])[:, lo:hi, :])

        def load_prior(b, lo=0, hi=PACK):
            if b not in prior_sb:
                prior_sb[b] = ring.tile([P, PACK, SPAN], BF16, name="prior_sb", bufs=4)
            nc.sync.dma_start(out=prior_sb[b][:, lo:hi, :], in_=rows(prior, b[0])[:, lo:hi, span(b[1], SPAN)])

        def load_near(b, lo=0, hi=PACK):
            key = (b[0], b[1] % C)
            if key not in near_sb:
                near_sb[key] = keep.tile([P, PACK, SPAN], BF16, name="near%d%d" % key)
            nc.sync.dma_start(out=near_sb[key][:, lo:hi, :], in_=rows(near, key[0])[:, lo:hi, span(key[1], SPAN)])

        def load_y(g, lo=0, hi=PACK):
            if g not in y_raw:
                y_raw[g] = ring.tile([P, PACK, R], BF16, name="y_raw")
            nc.sync.dma_start(out=y_raw[g][:, :, lo * P:hi * P], in_=rows(y, g)[:, :, lo * P:hi * P])

        def load_v():
            for r in range(PACK):
                nc.sync.dma_start(out=v_plane[r:P:32, :, :].bitcast(I32),
                                  in_=v_scales[:, r:16:PACK, :].rearrange("g q n -> q g n").bitcast(I32))
            nc.sync.dma_start(out=v_codes[:].bitcast(I32), in_=v_words.rearrange("g p n -> p g n").bitcast(I32))

        def quantize(key, src, cols, bufs):
            if key not in codes:
                width = src.shape[1] // PACK
                codes[key] = ring.tile([P, width], U32, name=key[0] + "_codes", bufs=bufs, align_bytes=64)
                scales[key] = ring.tile([P, width], U8, name=key[0] + "_scales", bufs=bufs, align_bytes=64)
            nc.vector.quantize_mx(out=codes[key][:, cols].bitcast(FP8X4), scales=scales[key][:, cols],
                                  in_=src[:, PACK * cols.start:PACK * cols.stop])

        def pieces(key, quarter):
            if key[0] == "left":
                return [(quarter, kk) for kk in range(K_PASSES)]
            return [(2 * (quarter // 2) + a, quarter % 2) for a in range(2)]

        def place(key, quarter):
            return quarter if key[0] == "left" else 2 * (quarter % 2) + quarter // 2

        def turn_proj(key, quarter, n):
            acc[key, quarter] = bank(n)
            for a, (slot, kk) in enumerate(pieces(key, quarter)):
                words = raw[key][:, slot, :].bitcast(F32)
                for u in range(2):
                    nc.tensor.transpose(acc[key, quarter][:, span(2 * a + u, P)],
                                        words[:, 2 * P * kk + u:2 * P * (kk + 1):2], ident[:])

        def stage_proj(key, quarter):
            if key not in staged:
                staged[key] = ring.tile([P, K_PASSES * SPAN * PACK], BF16, name="staged", align_bytes=64)
            dst = staged[key][:].bitcast(F32)[:, span(place(key, quarter), SPAN)]
            order = "p a r u" if key[0] == "left" else "p r a u"
            nc.scalar.copy(out=dst.rearrange("p (%s) -> %s" % (order[2:], order), a=2, u=2),
                           in_=acc[key, quarter][:].rearrange("p (a u r) -> " + order, a=2, u=2))

        def quantize_proj(key, lo, hi):
            quantize(key, staged[key], slice(2 * P * lo, 2 * P * hi), LIG if key[0] == "left" else REC)

        def mx(out, a, a_cols, b, b_cols, start, stop):
            nc.tensor.matmul_mx(out=out[:], lhsT=codes[a][:, a_cols].bitcast(FP8X4), lhsT_scale=scales[a][:, a_cols],
                                rhs=codes[b][:, b_cols].bitcast(FP8X4), rhs_scale=scales[b][:, b_cols],
                                start=start, stop=stop)

        def pair_matmul(b, t, n):
            acc[b, t] = bank(n)
            for kk in range(K_PASSES):
                mx(acc[b, t], ("left", b[0]), span(K_PASSES * t + kk, P), ("right", b[1]), span(kk, SPAN),
                   kk == 0, kk == K_PASSES - 1)

        def add_prior(b, t):
            if (b, t // 2) not in summed:
                summed[b, t // 2] = ring.tile([P, 2, SPAN], F32, name="summed%d" % (t // 2), bufs=2 - t // 2)
            nc.vector.tensor_tensor(out=summed[b, t // 2][:, t % 2, :].rearrange("p (h q e) -> p h q e", h=2, e=2),
                                    in0=acc[b, t][:].rearrange("p (h q e) -> p h q e", h=2, e=2),
                                    in1=prior_sb[b][:, t, :].rearrange("p (q h e) -> p h q e", h=2, e=2), op=ALU.add)

        spilled = {}

        def spill(b, t):
            spilled[b] = ring.tile([P, SPAN], F32, name="spilled")
            nc.scalar.copy(out=spilled[b][:], in_=acc[b, t][:])

        def add_prior_gpsimd(b, t):
            if (b, t // 2) not in summed:
                summed[b, t // 2] = ring.tile([P, 2, SPAN], F32, name="summed%d" % (t // 2), bufs=2 - t // 2)
            nc.gpsimd.tensor_tensor(out=summed[b, t // 2][:, t % 2, :].rearrange("p (h q e) -> p h q e", h=2, e=2),
                                    in0=spilled[b][:].rearrange("p (h q e) -> p h q e", h=2, e=2),
                                    in1=prior_sb[b][:, t, :].rearrange("p (q h e) -> p h q e", h=2, e=2), op=ALU.add)

        def gate(b, slots, h):
            if b not in paired:
                paired[b] = ring.tile([P, PACK, SPAN], BF16, name="paired", bufs=3)
            for t in slots:
                nc.vector.scalar_tensor_tensor(
                    out=paired[b][:, t, span(h, 2 * P)].rearrange("p (q e) -> p q e", e=2),
                    in0=summed[b, t // 2][:, t % 2, span(h, 2 * P)].rearrange("p (q e) -> p q e", e=2), scalar=0.0,
                    in1=near_sb[b[0], b[1] % C][:, t, :].rearrange("p (q h e) -> p h q e", h=2, e=2)[:, h, :, :],
                    op0=ALU.max, op1=ALU.mult)

        def turn_pair(b, u, n):
            acc[b, "turned", u] = bank(n)
            words = paired[b][:].bitcast(F32)
            for a in range(2):
                for h in range(2):
                    nc.tensor.transpose(acc[b, "turned", u][:, span(2 * a + h, P)], words[:, 2 * u + a, span(h, P)], ident[:])

        def stage_along_m(b, u):
            if b not in along_m:
                along_m[b] = ring.tile([P, SPAN * PACK], BF16, name="along_m", align_bytes=64)
            nc.scalar.copy(out=along_m[b][:].bitcast(F32)[:, span(u, SPAN)].rearrange("q (a p h) -> q a p h", a=2, h=2),
                           in_=acc[b, "turned", u][:].rearrange("q (a h p) -> q a p h", a=2, h=2))

        def stage_along_i(b, h, lo, hi, copy):
            if b not in along_i:
                along_i[b] = ring.tile([P, SPAN * PACK], BF16, name="along_i", align_bytes=64)
            copy(out=along_i[b][:, span(h, 2 * SPAN)].rearrange("p (e q t) -> p e q t", e=2, t=PACK)[:, lo:hi, :, :],
                 in_=paired[b][:, :, span(h, 2 * P)].rearrange("p t (q e) -> p e q t", e=2)[:, lo:hi, :, :])

        def quantize_along_i(b, lo, hi):
            quantize(("zi", b), along_i[b], slice(lo * P, hi * P), ZI_BUFS)

        def quantize_along_m(b, lo, hi):
            quantize(("zm", b), along_m[b], slice(lo * P, hi * P), ZM_BUFS)

        def stage_y(g, lo, hi, copy):
            if g not in y_staged:
                y_staged[g] = ring.tile([P, R * PACK], BF16, name="y_staged", align_bytes=64)
            cols = slice(lo * P, hi * P)
            copy(out=y_staged[g][:].rearrange("p (r t) -> p r t", t=PACK)[:, cols, :],
                 in_=y_raw[g][:].rearrange("p t r -> p r t")[:, cols, :])

        def quantize_y(g, lo=0, hi=PACK):
            quantize(("y", g), y_staged[g], slice(lo * P, hi * P), LIG)

        def keep_busy(count, key, width, n):
            idle = bank(n)
            for repeat in range(count):
                mx(idle[:, 0:width], key, slice(0, P), key, slice(0, width), True, True)

        def ligand_passes(g, t, chunks, start, stop, own_bank=None):
            if start:
                acc["lig", g, t] = bank(own_bank)
            for n in chunks:
                key = ("zm", (g, n))
                nc.tensor.matmul_mx(out=acc["lig", g, t][:], lhsT=codes[key][:, span(t, P)].bitcast(FP8X4),
                                    lhsT_scale=scales[key][:, span(t, P)],
                                    rhs=v_codes[:, n, :].bitcast(FP4X4), rhs_scale=v_plane[:, n, :],
                                    start=start and n == chunks[0], stop=stop and n == chunks[-1])

        def receptor_passes(n, s, own_bank):
            acc["rec", n, s] = bank(own_bank)
            for g in range(LIG):
                mx(acc["rec", n, s], ("zi", (g, n)), span(s, P), ("y", g), slice(0, R), g == 0, g == LIG - 1)

        res = {}

        def emit(kind, n, slot, copy):
            key = (kind, n, slot // 2)
            if key not in res:
                res[key] = ring.tile([P, 2, R], F32, name="res", bufs=4)
            copy(out=res[key][:, slot % 2, :], in_=acc[kind, n, slot][:])

        def store(kind, n, half):
            nc.sync.dma_start(out=rows(out_0 if kind == "lig" else out_1, n)[:, span(half, 2), :], in_=res[kind, n, half][:])

        on_scalar, on_vector = nc.scalar.copy, nc.vector.tensor_copy

        def on_gpsimd(out, in_):
            nc.gpsimd.tensor_scalar(out=out, in0=in_, scalar1=1.0, scalar2=0.0, op0=ALU.mult, op1=ALU.add)

        load_proj(("right", 0), 0, 2)
        turn_proj(("right", 0), 0, 2)
        load_proj(("right", 0), 2, 4)
        turn_proj(("right", 0), 1, 5)
        turn_proj(("right", 0), 2, 7)
        turn_proj(("right", 0), 3, 0)
        stage_proj(("right", 0), 0)
        stage_proj(("right", 0), 3)
        load_proj(("left", 0), 2, 4)
        turn_proj(("left", 0), 2, 4)
        quantize_proj(("right", 0), 0, 1)
        stage_proj(("right", 0), 2)
        load_proj(("left", 0), 0, 2)
        stage_proj(("right", 0), 1)
        stage_proj(("left", 0), 2)
        load_prior((0, 0))
        keep_busy(2, ("right", 0), 256, 2)
        load_y(0)
        load_proj(("right", 2), 2, 4)
        quantize_proj(("right", 0), 1, 2)
        load_proj(("right", 2), 0, 2)
        keep_busy(3, ("right", 0), 256, 0)
        turn_proj(("left", 0), 0, 5)
        quantize_proj(("right", 0), 2, 3)
        turn_proj(("left", 0), 1, 6)
        quantize_proj(("right", 0), 3, 4)
        quantize_proj(("left", 0), 2, 3)
        stage_proj(("left", 0), 0)
        stage_proj(("left", 0), 1)
        turn_proj(("left", 0), 3, 1)
        quantize_proj(("left", 0), 0, 1)
        pair_matmul((0, 0), 2, 3)
        stage_proj(("left", 0), 3)
        quantize_proj(("left", 0), 1, 2)
        pair_matmul((0, 0), 0, 0)
        add_prior((0, 0), 2)
        load_near((0, 0), 0, 2)
        quantize_proj(("left", 0), 3, 4)
        pair_matmul((0, 0), 1, 4)
        add_prior((0, 0), 0)
        turn_proj(("right", 2), 2, 1)
        stage_y(0, 0, 2, on_scalar)
        turn_proj(("right", 2), 0, 2)
        load_proj(("left", 1), 0, 2)
        add_prior((0, 0), 1)
        load_proj(("left", 1), 2, 4)
        turn_proj(("right", 2), 1, 5)
        turn_proj(("right", 2), 3, 3)
        stage_y(0, 2, 4, on_scalar)
        stage_proj(("right", 2), 0)
        stage_proj(("right", 2), 2)
        load_near((0, 0), 2, 4)
        stage_proj(("right", 2), 3)
        gate((0, 0), [0, 1], 0)
        pair_matmul((0, 0), 3, 4)
        turn_proj(("left", 1), 0, 2)
        gate((0, 0), [0, 1], 1)
        quantize_y(0)
        load_prior((0, 2))
        turn_proj(("left", 1), 1, 1)
        turn_proj(("left", 1), 2, 3)
        quantize_proj(("right", 2), 0, 2)
        load_proj(("right", 1), 0, 4)
        add_prior((0, 0), 3)
        stage_proj(("right", 2), 1)
        stage_proj(("left", 1), 0)
        quantize_proj(("right", 2), 2, 4)
        gate((0, 0), [2, 3], 1)
        load_y(1)
        pair_matmul((0, 2), 2, 7)
        stage_proj(("left", 1), 2)
        pair_matmul((0, 2), 0, 0)
        load_prior((1, 0))
        stage_proj(("left", 1), 1)
        gate((0, 0), [2, 3], 0)
        pair_matmul((0, 2), 3, 4)
        add_prior((0, 2), 2)
        stage_along_i((0, 0), 1, 0, 2, on_gpsimd)
        add_prior((0, 2), 0)
        turn_proj(("left", 1), 3, 5)
        turn_pair((0, 0), 0, 0)
        add_prior((0, 2), 3)
        turn_pair((0, 0), 1, 1)
        stage_along_i((0, 0), 0, 0, 2, on_scalar)
        pair_matmul((0, 2), 1, 3)
        turn_proj(("right", 1), 3, 7)
        stage_proj(("left", 1), 3)
        stage_along_m((0, 0), 1)
        gate((0, 2), [2, 3], 0)
        gate((0, 2), [2, 3], 1)
        stage_along_m((0, 0), 0)
        load_proj(("right", 3), 0, 4)
        turn_proj(("right", 1), 0, 5)
        quantize_proj(("left", 1), 0, 4)
        add_prior((0, 2), 1)
        turn_proj(("right", 1), 1, 4)
        gate((0, 2), [0, 1], 1)
        pair_matmul((1, 0), 0, 6)
        stage_y(1, 2, 4, on_scalar)
        stage_proj(("right", 1), 3)
        pair_matmul((1, 0), 3, 3)
        stage_proj(("right", 1), 0)
        pair_matmul((1, 0), 2, 2)
        turn_proj(("right", 1), 2, 0)
        load_near((1, 0))
        stage_proj(("right", 1), 1)
        pair_matmul((1, 0), 1, 5)
        quantize_along_m((0, 0), 0, 4)
        turn_proj(("right", 3), 2, 4)
        gate((0, 2), [0, 1], 0)
        stage_proj(("right", 1), 2)
        quantize_along_i((0, 0), 0, 4)
        stage_along_i((0, 2), 1, 0, 2, on_gpsimd)
        turn_proj(("right", 3), 3, 7)
        add_prior((1, 0), 2)
        stage_y(1, 0, 2, on_scalar)
        add_prior((1, 0), 3)
        add_prior((1, 0), 0)
        turn_proj(("right", 3), 1, 6)
        quantize_proj(("right", 1), 0, 4)
        add_prior((1, 0), 1)
        stage_proj(("right", 3), 2)
        gate((1, 0), [0, 1], 0)
        pair_matmul((0, 1), 3, 3)
        stage_proj(("right", 3), 3)
        gate((1, 0), [2, 3], 0)
        load_prior((0, 1))
        stage_proj(("right", 3), 1)
        spill((0, 1), 3)
        turn_proj(("right", 3), 0, 1)
        turn_pair((0, 2), 1, 2)
        turn_pair((0, 2), 0, 6)
        gate((1, 0), [0, 1], 1)
        stage_proj(("right", 3), 0)
        pair_matmul((0, 1), 0, 0)
        gate((1, 0), [2, 3], 1)
        quantize_proj(("right", 3), 0, 4)
        stage_along_m((0, 2), 1)
        pair_matmul((0, 1), 1, 5)
        stage_along_m((0, 2), 0)
        stage_along_i((1, 0), 1, 0, 2, on_scalar)
        pair_matmul((0, 1), 2, 4)
        turn_pair((1, 0), 1, 1)
        pair_matmul((0, 3), 2, 2)
        stage_along_i((0, 2), 0, 0, 2, on_scalar)
        load_v()
        add_prior((0, 1), 1)
        add_prior((0, 1), 0)
        add_prior((0, 1), 2)
        pair_matmul((1, 2), 3, 6)
        add_prior_gpsimd((0, 1), 3)
        load_near((0, 1))
        quantize_y(1)
        gate((0, 1), [2, 3], 1)
        pair_matmul((1, 1), 1, 5)
        stage_along_i((1, 0), 0, 0, 2, on_scalar)
        load_prior((1, 1))
        load_prior((0, 3))
        load_prior((1, 3))
        gate((0, 1), [0, 1], 0)
        pair_matmul((0, 3), 3, 3)
        load_near((1, 1))
        gate((0, 1), [0, 1], 1)
        pair_matmul((0, 3), 0, 7)
        stage_along_m((1, 0), 1)
        turn_pair((0, 1), 0, 4)
        pair_matmul((0, 3), 1, 0)
        quantize_along_i((1, 0), 0, 4)
        load_prior((1, 2))
        spill((1, 2), 3)
        quantize_along_m((0, 2), 0, 4)
        gate((0, 1), [2, 3], 0)
        receptor_passes(0, 1, 1)
        add_prior((0, 3), 1)
        spill((0, 3), 3)
        add_prior((0, 3), 0)
        turn_pair((0, 1), 1, 6)
        add_prior((0, 3), 2)
        stage_along_m((0, 1), 0)
        turn_pair((1, 0), 0, 4)
        receptor_passes(0, 2, 3)
        pair_matmul((1, 2), 0, 7)
        add_prior((1, 1), 1)
        add_prior_gpsimd((0, 3), 3)
        receptor_passes(0, 3, 2)
        gate((0, 3), [2, 3], 0)
        gate((0, 3), [0, 1], 0)
        emit("rec", 0, 1, on_scalar)
        stage_along_m((0, 1), 1)
        receptor_passes(0, 0, 1)
        emit("rec", 0, 2, on_scalar)
        stage_along_m((1, 0), 0)
        emit("rec", 0, 3, on_scalar)
        pair_matmul((1, 1), 2, 6)
        emit("rec", 0, 0, on_scalar)
        gate((0, 3), [0, 1], 1)
        quantize_along_i((0, 2), 0, 4)
        pair_matmul((1, 2), 1, 3)
        gate((0, 3), [2, 3], 1)
        quantize_along_m((1, 0), 0, 4)
        pair_matmul((1, 2), 2, 0)
        stage_along_i((0, 1), 1, 0, 2, on_scalar)
        add_prior((1, 2), 2)
        add_prior((1, 2), 1)
        turn_pair((0, 3), 1, 5)
        turn_pair((0, 3), 0, 2)
        stage_along_m((0, 3), 1)
        add_prior((1, 2), 0)
        stage_along_m((0, 3), 0)
        pair_matmul((1, 3), 0, 4)
        add_prior_gpsimd((1, 2), 3)
        quantize_along_m((0, 1), 0, 4)
        gate((1, 2), [0, 1], 0)
        gate((1, 2), [2, 3], 0)
        gate((1, 2), [0, 1], 1)
        stage_along_i((0, 3), 0, 0, 2, on_scalar)
        store("rec", 0, 1)
        stage_along_i((0, 1), 0, 0, 2, on_scalar)
        pair_matmul((1, 1), 3, 1)
        gate((1, 2), [2, 3], 1)
        pair_matmul((1, 1), 0, 5)
        ligand_passes(0, 0, [0, 2, 1], True, False, 0)
        quantize_along_i((0, 1), 0, 4)
        quantize_along_m((0, 3), 0, 4)
        stage_along_i((0, 3), 1, 0, 2, on_scalar)
        ligand_passes(0, 2, [0, 2, 1], True, False, 7)
        add_prior((1, 1), 0)
        add_prior((1, 1), 3)
        ligand_passes(0, 1, [0, 2, 1], True, False, 3)
        ligand_passes(0, 3, [0, 2, 1, 3], True, True, 2)
        add_prior((1, 1), 2)
        stage_along_i((1, 2), 1, 0, 2, on_gpsimd)
        ligand_passes(0, 2, [3], False, True)
        stage_along_i((1, 2), 0, 0, 2, on_scalar)
        gate((1, 1), [0, 1], 0)
        emit("lig", 0, 2, on_scalar)
        turn_pair((1, 2), 0, 5)
        quantize_along_i((1, 2), 0, 4)
        turn_pair((1, 2), 1, 1)
        emit("lig", 0, 3, on_scalar)
        gate((1, 1), [0, 1], 1)
        stage_along_m((1, 2), 0)
        ligand_passes(0, 0, [3], False, True)
        store("rec", 0, 0)
        gate((1, 1), [2, 3], 0)
        pair_matmul((1, 3), 1, 7)
        quantize_along_i((0, 3), 0, 4)
        stage_along_m((1, 2), 1)
        gate((1, 1), [2, 3], 1)
        pair_matmul((1, 3), 2, 2)
        stage_along_i((1, 1), 1, 0, 2, on_gpsimd)
        emit("lig", 0, 0, on_scalar)
        receptor_passes(2, 1, 5)
        ligand_passes(0, 1, [3], False, True)
        pair_matmul((1, 3), 3, 1)
        emit("rec", 2, 1, on_scalar)
        turn_pair((1, 1), 0, 0)
        turn_pair((1, 1), 1, 5)
        store("lig", 0, 1)
        add_prior((1, 3), 0)
        add_prior((1, 3), 3)
        emit("lig", 0, 1, on_scalar)
        stage_along_i((1, 1), 0, 0, 2, on_scalar)
        add_prior((1, 3), 2)
        receptor_passes(2, 3, 6)
        quantize_along_i((1, 1), 0, 4)
        gate((1, 3), [2, 3], 0)
        receptor_passes(2, 2, 4)
        store("lig", 0, 0)
        emit("rec", 2, 3, on_scalar)
        receptor_passes(2, 0, 3)
        receptor_passes(1, 1, 6)
        stage_along_m((1, 1), 0)
        receptor_passes(1, 2, 0)
        add_prior((1, 3), 1)
        receptor_passes(1, 3, 1)
        stage_along_m((1, 1), 1)
        emit("rec", 2, 0, on_scalar)
        gate((1, 3), [0, 1], 0)
        emit("rec", 2, 2, on_scalar)
        quantize_along_m((1, 2), 0, 4)
        receptor_passes(1, 0, 7)
        quantize_along_m((1, 1), 0, 4)
        stage_along_i((1, 3), 0, 0, 2, on_scalar)
        emit("rec", 1, 2, on_vector)
        ligand_passes(1, 0, [0, 2], True, False, 3)
        emit("rec", 1, 3, on_scalar)
        ligand_passes(1, 3, [0, 2], True, False, 5)
        store("rec", 2, 0)
        quantize_along_i((1, 3), 0, 2)
        gate((1, 3), [0, 1], 1)
        ligand_passes(1, 0, [1], False, False)
        store("rec", 2, 1)
        emit("rec", 1, 0, on_scalar)
        ligand_passes(1, 3, [1], False, False)
        receptor_passes(3, 0, 0)
        turn_pair((1, 3), 0, 2)
        store("rec", 1, 1)
        gate((1, 3), [2, 3], 1)
        emit("rec", 1, 1, on_scalar)
        stage_along_m((1, 3), 0)
        stage_along_i((1, 3), 1, 0, 1, on_vector)
        stage_along_i((1, 3), 1, 1, 2, on_vector)
        turn_pair((1, 3), 1, 1)
        store("rec", 1, 0)
        quantize_along_m((1, 3), 0, 2)
        receptor_passes(3, 1, 7)
        emit("rec", 3, 1, on_vector)
        emit("rec", 3, 0, on_scalar)
        stage_along_m((1, 3), 1)
        ligand_passes(1, 1, [0, 2], True, False, 4)
        ligand_passes(1, 1, [1], False, False)
        quantize_along_i((1, 3), 2, 4)
        ligand_passes(1, 1, [3], False, True)
        ligand_passes(1, 0, [3], False, True)
        emit("lig", 1, 1, on_scalar)
        store("rec", 3, 0)
        receptor_passes(3, 2, 1)
        receptor_passes(3, 3, 2)
        emit("rec", 3, 2, on_scalar)
        quantize_along_m((1, 3), 2, 4)
        ligand_passes(1, 3, [3], False, True)
        emit("rec", 3, 3, on_scalar)
        ligand_passes(1, 2, [0, 2], True, False, 0)
        emit("lig", 1, 0, on_vector)
        emit("lig", 1, 3, on_scalar)
        store("lig", 1, 0)
        ligand_passes(1, 2, [1], False, False)
        ligand_passes(1, 2, [3], False, True)
        store("rec", 3, 1)
        emit("lig", 1, 2, on_scalar)
        store("lig", 1, 1)
